import numpy as np, ml_dtypes
CORES = [2,6,10,14,18,22,26,30]
N = 8
BF = ml_dtypes.bfloat16
def gentries(a):
    return np.ascontiguousarray(a.reshape(8, 16, -1).transpose(0, 2, 1)).reshape(8, -1)
def gtable(e):
    e = np.asarray(e); return np.ascontiguousarray(e.reshape(8, -1, 16).transpose(0, 2, 1)).reshape(128, -1).astype(np.int32)
R, F, C, D, B = 16384, 4096, 512, 1, 1 << 20
def passing(at, lim):
    a0 = at[:, 0].reshape(8, R); l = lim.reshape(8, 2)
    return (a0 >= l[:, :1]) & (a0 <= l[:, 1:])
def dims(rng, m, w, first=None):
    lo = rng.integers(-(B >> 1), B >> 2, (8, 1)); hi = lo + w[:, None]; z = rng.random((8, R))
    if first is not None: z[np.arange(8), first] = -1
    ok = np.argsort(np.argsort(z, 1), 1) < m[:, None]
    out = np.where(rng.random((8, R)) < 0.5, rng.integers(1 - B, lo, (8, R)), rng.integers(hi + 1, B, (8, R)))
    return lo, hi, ok, np.where(ok, rng.integers(lo, hi + 1, (8, R)), out)
def living(n, z):
    return np.argsort(np.argsort(z, 1), 1) < n[:, None]
def facts(rng, ok, live, p, where, e=1):
    m = np.sum(ok, axis=1)[:, None]; o = np.argsort(~ok, 1, kind="stable")
    bad = rng.random((N, 8, F)) < p; np.put_along_axis(bad, where, True, 1); bad = bad & ~live[:, None]
    k = np.where(bad, R - m, m); j = np.minimum((rng.random((N, 8, F)) ** e * k).astype(np.int64), k - 1)
    return o[np.arange(8)[:, None], j + np.where(bad, m, 0)]
def pack(lo, hi, v, rest, fk, me):
    rest[:, 0] = v
    return {"at": np.ascontiguousarray(rest.reshape(N, D, 16, R).transpose(0, 2, 1, 3)).reshape(N, 16, D * R).astype(np.int32),
            "lim": np.concatenate([lo, hi], 1).reshape(N, 1, 2 * D).astype(np.int32), "fk": np.stack([gtable(x) for x in fk]), "me": me.reshape(N, 1, F).astype(np.int32)}
def whole(rng, *shape):
    return rng.integers(1 - B, B, shape)
def setup_inputs(rng):
    lo, hi, ok, v = dims(rng, rng.integers(R // 4, 3 * R // 4, 8), rng.integers(B >> 6, B >> 2, 8))
    live = living(rng.integers(C // 4, C, N), rng.random((N, F)))
    return pack(lo, hi, v, whole(rng, 8, 16, R), facts(rng, ok, live, 0.15, rng.integers(0, 8, (N, 1, F))), whole(rng, N, F))
def setup_inputs_full(rng):
    lo, hi, ok, v = dims(rng, rng.integers(R // 4, 3 * R // 4, 8), rng.integers(B >> 6, B >> 2, 8))
    n = np.full(N, C); n[rng.integers(0, N)] = 1; z = rng.random((N, F)); z[:, 0] = -1; z[:, -1] = -2
    return pack(lo, hi, v, whole(rng, 8, 16, R), facts(rng, ok, living(n, z), 0.3, rng.integers(0, 8, (N, 1, F))), whole(rng, N, F))
def setup_inputs_ends(rng):
    w = np.where(rng.permutation(8) < 3, 0, rng.integers(1, 1000, 8))
    lo, hi, ok, v = dims(rng, rng.integers(R // 4, 3 * R // 4, 8), w); h = rng.random((8, R)) < 0.5
    v = np.where(ok, np.where(h, lo, hi), np.where(h, lo - 1, hi + 1)); j = np.arange(F)
    live = living(rng.integers(C // 4, C + 1, N), np.minimum(j, F - 1 - j)[None] + np.zeros((N, 1)))
    return pack(lo, hi, v, whole(rng, 8, 16, R), facts(rng, ok, live, 0.1, rng.integers(0, 8, (N, 1, F))), whole(rng, N, F))
def setup_inputs_alike(rng):
    m = np.where(rng.permutation(8) < 4, 1, R - 1)
    lo, hi, ok, v = dims(rng, m, rng.integers(0, B >> 2, 8), np.where(rng.random(8) < 0.5, 0, R - 1))
    live = living(rng.integers(C // 4, C + 1, N), rng.random((N, F))); fk = facts(rng, ok, live, 0.1, rng.integers(0, 8, (N, 1, F)))
    q = rng.integers(0, N); s = np.flatnonzero(live[q]); fk[q][:, s] = fk[q][:, s[:1]]
    return pack(lo, hi, v, whole(rng, 8, 16, R), fk, whole(rng, N, F))
def setup_inputs_near(rng):
    lo, hi, ok, v = dims(rng, rng.integers(R // 4, 3 * R // 4, 8), rng.integers(B >> 6, B >> 2, 8))
    where = np.where(rng.random((N, 1, 1)) < 0.5, rng.integers(0, 8, (N, 1, 1)), rng.integers(0, 8, (N, 1, F)))
    live = living(rng.integers(C // 4, C + 1, N), rng.random((N, F))); sg = rng.choice(np.array([-1, 1]), (1, 16, 1))
    rest = sg * (B - 1 - rng.integers(0, 50, (8, 16, R))); me = rng.choice(np.array([-1, 1]), (N, 1)) * (B - 1 - rng.integers(0, 50, (N, F)))
    return pack(lo, hi, v, rest, facts(rng, ok, live, 0.0, where), me)
def setup_inputs_spread(rng):
    lo, hi, ok, v = dims(rng, np.maximum(1, R >> rng.integers(1, 10, 8)), 1 << rng.integers(0, 18, 8))
    live = living(np.maximum(1, C >> rng.integers(0, 6, N)), rng.random((N, F)))
    rest = whole(rng, 8, 16, R) >> rng.integers(0, 20, (8, 16, R)); me = whole(rng, N, F) >> rng.integers(0, 20, (N, F))
    return pack(lo, hi, v, rest, facts(rng, ok, live, rng.random((1, 8, 1)), rng.integers(0, 8, (N, 1, F)), 4), me)
def check_inputs(d):
    bad = [k for k in ("at", "lim", "me") if not ((d[k] > -B) & (d[k] < B)).all()]
    if not ((d["fk"] >= 0) & (d["fk"] < R)).all(): return bad + ["fk"]
    ok = passing(d["at"], d["lim"]); g = np.arange(8)[:, None]
    n = [int(np.sum(np.all(ok[g, gentries(a)], axis=0))) for a in d["fk"]]
    return bad + ([] if min(n) >= 1 and max(n) <= C else ["survivors"])
def reference(at, lim, fk, me):
    y = np.zeros((N, 16, C + 1), np.int64); ok = passing(at, lim); g = np.arange(8)[:, None]
    a = np.ascontiguousarray(at.reshape(N, 16, D, R).transpose(0, 2, 1, 3)).reshape(8, 16, R).astype(np.int64)
    for r in range(N):
        k = gentries(fk[r]); s = np.flatnonzero(np.all(ok[g, k], axis=0)); n = len(s)
        y[r, :, :n] = me[r, 0][s][None]
        for d in range(8): y[r, :, :n] += a[d][:, k[d, s]]
        y[r, :, C] = n
    return {"y": np.asarray(y, np.float32)}

@@ -1,0 +1,481 @@
+import math
+from concourse.bass import DstId, RemoteDMATransfer
+from concourse.mybir import AluOpType as A, ActivationFunctionType as Fn
+
+F32, BF, I32, U16 = "float32", "bfloat16", "int32", "uint16"
+WIN = 5120
+ROWS = 16384
+PARTS = (1920, 1792, 1792)
+OWN = ROWS - sum(PARTS)
+SCRATCH = {}
+for _t, _list in (
+        (BF, "f1 128,f2 128,pall 136,onesb 128,negb 128,m16 16,wp 16,idb 128,tri 128,qs0 8,qs 8,"
+             "bb 256,rb 256,vb 512,win8 1024,gw 4096,tt 128,sc 128,msk 128,cum 32,win 5120,sel 8,selh 8,"
+             "lh00 128,lh01 128,lh10 128,lh11 128,hl0 256,hl1 256"),
+        (I32, "a0 128,im 16,im2 16,im8 8,gi 1,fks 256,wi 256,bi 256,u0 128,u1 128,v0 128,v1 128,mn 512,"
+              "ml 32,ml2 32,at2 16392,vr 256,vh 256,vl 256,hw 1920"),
+        (F32, "onesf 128,m8f 8,gf 1,gpf 1,xj 32,rt 256,e1 32,e2 32,ga 512,rx3 448,q1 128,q2 64,q3 64,qm 64,qf 64,qg 64,"
+              "mv 512,mwin 5120,b7 240,yo 68"),
+        (U16, "w16 256,off 32,off2 32,offo 8,ml16 32,z16 32")):
+    for _x in _list.split(","):
+        SCRATCH[_x.split()[0]] = ("sbuf", [128, int(_x.split()[1])], _t)
+for _k in range(3):
+    SCRATCH["hd%d" % _k] = ("dram", [2, 128, PARTS[_k] // 16], I32)
+    SCRATCH["raw%d" % _k] = ("sbuf", [128, PARTS[_k] // 8], I32)
+SCRATCH["lm"] = ("sbuf", [1, 2], I32)
+SCRATCH["lf"] = ("sbuf", [1, 2], F32)
+for _k in range(8):
+    SCRATCH["p%d" % _k] = ("psum", [128, 512], F32)
+SEMAPHORES = ["x1", "x2", "x3a", "x3b", "x3c", "l0", "l1", "l2", "l3", "hr", "wn"] + ["e%d" % k for k in range(130)]
+
+
+def helpers(core, T, topo):
+    hs = [c for c in topo.cores_of(core) if c not in T.cores and topo.die(c) == topo.die(core)]
+    return hs[:len(PARTS)]
+
+
+def part_start(i, t=0):
+    return 1 + OWN + sum(PARTS[:i]) + t * PARTS[i] // 2
+
+
+def distance_order(core, T, topo):
+    here = topo.chip(core)
+    chips = []
+    for c in T.cores:
+        if topo.chip(c) not in chips:
+            chips.append(topo.chip(c))
+
+    def far(ch):
+        if ch == here:
+            return 0
+        if topo.mates(ch, here):
+            return 1
+        return 2 if topo.same_plane(ch, here) else 3
+    out = []
+    for ch in sorted(chips, key=lambda ch: (-far(ch), (ch - here) % len(chips))):
+        out.append((ch, [r for r in range(len(T.cores)) if topo.chip(T.cores[r]) == ch]))
+    return out
+
+
+def slot_of(rank, sender, T, topo):
+    flat = [r for ch, rs in distance_order(T.cores[rank], T, topo) for r in rs if r != rank] + [rank]
+    return flat.index(sender)
+
+
+def engine_sets(core, T, topo):
+    me = T.rank_of(core)
+    order = distance_order(core, T, topo)
+    near = [r for r in order[-1][1] if r != me]
+    eo = topo.engines(core, T.cores[order[0][1][0]])
+    return eo, [e for e in topo.engines(core, T.cores[near[0]]) if e not in eo]
+
+
+def helper_engines(core, T, topo):
+    eo, en = engine_sets(core, T, topo)
+    return [[eo, en], [eo[:4], eo[4:]], [en[:4], en[4:]]]
+
+
+def plans(core, T, topo):
+    me = T.rank_of(core)
+    order = distance_order(core, T, topo)
+    far = [r for ch, rs in order[:-1] for r in rs]
+    near = [r for r in order[-1][1] if r != me]
+    eo, en = engine_sets(core, T, topo)
+    x1 = [[(far, eo), (near, en[:2])]]
+    x2 = [[([far[k]], eo[2 * k:2 * k + 2]) for k in range(4)] + [(near, en[:2])],
+          [([far[4 + k]], eo[4 * k:4 * k + 4]) for k in range(2)]]
+    x3 = [[([far[k]], eo[2 * k:2 * k + 2]) for k in range(4)],
+          [([far[4 + k]], eo[4 * k:4 * k + 4]) for k in range(2)] + [(near, en[:4])]]
+    return order, x1, x2, x3
+
+
+def arriving(core, T, topo, which, slots=range(8)):
+    me, n = T.rank_of(core), 0
+    for c in T.cores:
+        if c != core and slot_of(me, T.rank_of(c), T, topo) in slots:
+            for call in plans(c, T, topo)[which]:
+                for dests, eng in call:
+                    if me in dests:
+                        n += len(eng)
+    return n
+
+
+def transfer(dest_cores, eng, rsem, src, dst, topo):
+    ids = []
+    for c in dest_cores:
+        rid, pid, se = topo.addr(c)
+        ids.append(DstId(rid=rid, pnc=pid))
+    return RemoteDMATransfer(dst_ids=ids, dma_engine_mask=sum(1 << e for e in eng), remote_sem=rsem, srcs=[src],
+                             dsts=[dst] * len(ids))
+
+
+def helper_program(g, core, T, topo):
+    owners = [c for c in T.cores if core in helpers(c, T, topo)]
+    if not owners:
+        return
+    owner = owners[0]
+    i = helpers(owner, T, topo).index(core)
+    n = PARTS[i] // 2
+    for q in (g.sync, g.scalar):
+        q.wait_ge(T.sem.hr, sum(len(e) for e in helper_engines(owner, T, topo)[i]))
+    for t in range(2):
+        for k in range(8):
+            q = (g.sync, g.scalar)[k % 2]
+            q.dma_start(T.hw[16 * k:16 * k + 16, n * t:n * t + n], T["hd%d" % i][t]).then_inc(T.sem["e%d" % t], 16)
+    eng = topo.engines(core, owner)
+    for t in range(2):
+        g.wait_ge(T.sem["e%d" % t], 128)
+        c0 = part_start(i, t)
+        g.remote_dma_fused([transfer([owner], eng, T.sem.wn, T.hw[:, n * t:n * t + n], T.at2[:, c0:c0 + n], topo)],
+                           local_sem=T.sem.l0)
+    g.wait_ge(T.sem.l0, 2 * len(eng))
+
+
+def rank_program(g, core, T, topo):
+    me = T.rank_of(core)
+    if me is None:
+        helper_program(g, core, T, topo)
+        return
+    V, S, P, Y = g.vector, g.scalar, g.tensor, g.sync
+    names = {"g": g, "V": V, "S": S, "P": P, "Y": Y}
+    evs = []
+    known = {k: [] for k in names}
+    waited = []
+
+    def ev():
+        evs.append(0)
+        return len(evs) - 1
+
+    def inc(e, ins, n=1):
+        ins.then_inc(T.sem["e%d" % e], n)
+        evs[e] += n
+        return e
+
+    def one(ins, n=1):
+        return inc(ev(), ins, n)
+
+    def w(qn, *es):
+        for e in es:
+            if e not in known[qn]:
+                names[qn].wait_ge(T.sem["e%d" % e], evs[e])
+                known[qn].append(e)
+                waited.append(e)
+
+    def mm(out, lhsT, rhs, start=True, stop=True):
+        return P.matmul(out, lhsT, rhs, start, stop)
+
+    def copy(qn, out, in_):
+        return V.tensor_copy(out, in_) if qn == "V" else S.activation(out, in_, Fn.Copy)
+
+    order, x1, x2, x3 = plans(core, T, topo)
+    n1, n2 = arriving(core, T, topo, 1), arriving(core, T, topo, 2)
+    n3a, n3b, n3c = [arriving(core, T, topo, 3, s) for s in (range(4), range(4, 6), range(6, 8))]
+    hs, heng = helpers(core, T, topo), helper_engines(core, T, topo)
+    nw = sum(2 * len(topo.engines(h, core)) for h in hs)
+    m0 = sum(len(e) for h in heng for e in h)
+
+    def send(calls, rsem, lsem, src, dst):
+        n = 0
+        for call in calls:
+            g.remote_dma_fused([transfer([T.cores[r] for r in dests], eng, rsem(dests[0]), src(dests[0]), dst(dests[0]),
+                                         topo) for dests, eng in call], local_sem=lsem)
+            n += sum(len(eng) for dests, eng in call)
+        return n
+
+    def raw(i, t):
+        n = PARTS[i] // 16
+        return T["raw%d" % i][:, n * t:n * t + n]
+
+    def send_raw(which):
+        g.remote_dma_fused([transfer([hs[i]], heng[i][t], T.sem.hr, raw(i, t), T["hd%d" % i][t], topo)
+                            for i in which for t in range(2)], local_sem=T.sem.l0)
+
+    def raw_load(q, i):
+        e = ev()
+        for t in range(2):
+            c0 = part_start(i, t) - 1
+            inc(e, q.dma_start(raw(i, t), T["at"][:, c0:c0 + PARTS[i] // 2]), 16)
+        return e
+
+    e_lim = one(S.dma_start(T.lm[:, :], T.lim[:, :]), 16)
+    e_a0 = one(Y.dma_start(T.a0[:, :], T["at"][0:1, :]), 16)
+    e_fk = one(S.dma_start(T.fks[:, :], T.fk[:, :]), 16)
+    e_raw = [raw_load(Y, 0)]
+    e_vr = ev()
+    for k in range(8):
+        inc(e_vr, Y.dma_start(T.vr[16 * k:16 * k + 16, :], T.fk[:, 32 * k:32 * k + 32]), 16)
+    e_raw += [raw_load(Y, 1), raw_load(Y, 2)]
+
+    e_im = one(g.iota(T.im[:, :], [[-1, 16]], 0, 1))
+    e_ml = one(g.iota(T.ml[:, :], [[1, 32]], 0, 32))
+    e_onesb = one(V.memset(T.onesb[:, :], 1.0))
+    e_onesf = one(V.memset(T.onesf[:, :], 1.0))
+    w("V", e_im)
+    e_gi = one(V.tensor_scalar(T.gi[:, :], T.im[:, 0:1], 3, 7, A.logical_shift_right, A.bitwise_and))
+    e_im8 = one(V.tensor_scalar(T.im8[:, :], T.im[:, 0:8], 7, None, A.bitwise_and))
+    w("V", e_gi)
+    e_gf = one(V.tensor_copy(T.gf[:, :], T.gi[:, :]))
+    w("S", e_gf)
+    e_gp = one(S.activation(T.gpf[:, :], T.gf[:, :], Fn.Exp, scale=math.log(2.0)))
+    e_im2 = one(V.tensor_scalar(T.im2[:, :], T.im[:, :], 15, None, A.bitwise_and))
+    w("V", e_im8)
+    e_m8f = one(V.tensor_scalar(T.m8f[:, :], T.im8[:, :], 0.0, None, A.is_equal))
+    e_wp = one(V.memset(T.wp[:, :], 0.0))
+    w("V", e_im2)
+    e_m16 = one(V.tensor_scalar(T.m16[:, :], T.im2[:, :], 0.0, None, A.is_equal))
+    w("V", e_ml)
+    e_ml2 = one(V.tensor_scalar(T.ml2[:, :], T.ml[:, :], 511, None, A.bitwise_and))
+    e_pt = one(V.memset(T.pall[:, 128:136], 0.0))
+    w("V", e_m16)
+    e_selh = one(V.tensor_scalar(T.selh[:, :], T.m16[:, 0::2], 128.0, None, A.mult))
+    w("V", e_ml2)
+    e_ml16 = one(V.tensor_copy(T.ml16[:, :], T.ml2[:, :]))
+    w("V", e_selh)
+    e_sel = one(V.tensor_tensor(T.sel[:, :], T.selh[:, :], T.m16[:, 1::2], A.add))
+    e_slot = one(V.memset(T.at2[:, 0:1], 0))
+    w("g", e_onesb)
+    e_id = one(g.affine_select(T.idb[:, :], T.onesb[:, :], [[-1, 128]], A.is_equal, 0.0, 0, 1))
+    e_tri = one(g.affine_select(T.tri[:, :], T.onesb[:, :], [[1, 128]], A.is_gt, 0.0, 0, -1))
+
+    w("g", e_raw[0])
+    send_raw([0])
+
+    w("V", e_lim)
+    e_lf = one(V.tensor_copy(T.lf[:, :], T.lm[:, :]))
+    w("P", e_lf, e_onesf)
+    e_lp = one(mm(T.p0[:, 0:2], T.onesf[0:1, :], T.lf[:, :]))
+    w("V", e_wp, e_m8f, e_gp)
+    e_w = ev()
+    for x in range(2):
+        s = slice(64 * x, 64 * x + 64)
+        inc(e_w, V.tensor_scalar(T.wp[s, 8 * x:8 * x + 8], T.m8f[s, :], T.gpf[s, 0:1], None, A.mult))
+    w("V", e_lp, e_a0)
+    e_f1 = one(V.tensor_scalar(T.f1[:, :], T.a0[:, :], T.p0[:, 0:1], None, A.is_lt))
+    e_f2 = one(V.tensor_scalar(T.f2[:, :], T.a0[:, :], T.p0[:, 1:2], None, A.is_gt))
+    w("P", e_w, e_f1)
+    mm(T.p7[:, 0:16], T.f1[:, :], T.wp[:, :], True, False)
+    w("P", e_f2)
+    e_pk = one(mm(T.p7[:, 0:16], T.f2[:, :], T.wp[:, :], False, True))
+    w("V", e_pk)
+    slot1 = T.pall[:, 16 * me:16 * me + 16]
+    e_pall = one(V.tensor_copy(slot1, T.p7[:, 0:16]))
+
+    w("g", e_pall)
+    m1 = send(x1, lambda r: T.sem.x1, T.sem.l1, lambda r: slot1, lambda r: slot1)
+    w("g", e_raw[1], e_raw[2])
+    send_raw([1, 2])
+
+    e_mn0 = one(g.iota(T.mn[:, :], [[0, 512]], 0, 0))
+    e_qs0 = one(g.affine_select(T.qs0[:, :], T.onesb[:, 0:8], [[-16, 8]], A.is_equal, 0.0, 0, 1))
+    w("g", e_qs0)
+    e_qs = one(g.affine_select(T.qs[:, :], T.qs0[:, :], [[-16, 8]], A.not_equal, 256.0, -8, 1))
+    e_lh = ev()
+    for x in range(2):
+        for hl in range(2):
+            inc(e_lh, g.affine_select(T["lh%d%d" % (x, hl)][:, :], T.onesb[:, :], [[-2, 64], [1000, 2]], A.is_equal, 0.0,
+                                      -x - 1000 * hl, 1))
+    e_msk = one(g.affine_select(T.msk[:, :], T.onesb[:, :], [[0, 32], [1, 4]], A.not_equal, 0.0, 0, 0))
+    e_xj = one(g.iota(T.xj[:, :], [[1, 32]], 513, 32, allow_small_or_imprecise_dtypes=True))
+    e_win0 = one(g.iota(T.win[:, 0:512], [[0, 512]], 0, 0, allow_small_or_imprecise_dtypes=True))
+    e_mw0 = one(g.iota(T.mwin[:, 0:512], [[0, 512]], 0, 0, allow_small_or_imprecise_dtypes=True))
+    e_negb = one(g.iota(T.negb[:, :], [[0, 128]], -1, 0, allow_small_or_imprecise_dtypes=True))
+    e_b70 = one(g.iota(T.b7[:, :], [[0, 240]], 1, 0, allow_small_or_imprecise_dtypes=True))
+    w("g", e_b70)
+    e_b7 = one(g.affine_select(T.b7[:, :], T.b7[:, :], [[1, 15], [0, 16]], A.is_equal, 0.0, -7, 0))
+
+    w("Y", e_slot)
+    Y.wait_ge(T.sem.l1, m1)
+    e_at = ev()
+    for k in range(8):
+        inc(e_at, Y.dma_start(T.at2[16 * k:16 * k + 16, 1:OWN + 1], T["at"][:, 0:OWN]), 16)
+        if k == 3:
+            w("Y", e_mn0)
+            e_mn = one(Y.dma_start(T.mn[0::16, :], T["me"][0:1, :]), 16)
+
+    w("V", e_fk)
+    e_bi = one(V.tensor_scalar(T.bi[:, :], T.fks[:, :], 10, None, A.arith_shift_right))
+    e_wi = one(V.tensor_scalar(T.wi[:, :], T.fks[:, :], 1023, None, A.bitwise_and))
+    w("V", e_bi)
+    e_bb = ev()
+    for h in range(2):
+        inc(e_bb, V.tensor_copy(T.bb[:, 128 * h:128 * h + 128], T.bi[:, h::2]))
+    w("V", e_wi)
+    e_w16 = ev()
+    for h in range(2):
+        inc(e_w16, V.tensor_copy(T.w16[:, 128 * h:128 * h + 128], T.wi[:, h::2]))
+    w("S", e_bb)
+    e_rb = one(S.activation(T.rb[:, :], T.bb[:, :], Fn.Exp, scale=-math.log(2.0)))
+    w("P", e_rb, e_id)
+    e_rp = ev()
+    for h in range(2):
+        for d in range(8):
+            inc(e_rp, mm(T.p1[:, 128 * h + d:128 * h + 128:8], T.rb[:, 128 * h:128 * h + 128],
+                         T.idb[:, 16 * d:16 * d + 16]))
+    w("S", e_rp)
+    e_rt = one(S.activation(T.rt[:, :], T.p1[:, 0:256], Fn.Copy, scale=32768.0))
+    w("V", e_vr)
+    e_vh = one(V.tensor_scalar(T.vh[:, :], T.vr[:, :], 7, None, A.arith_shift_right))
+    e_vl = one(V.tensor_scalar(T.vl[:, :], T.vr[:, :], 127, None, A.bitwise_and))
+    e_hl = ev()
+    w("V", e_vh)
+    for h in range(2):
+        inc(e_hl, V.tensor_copy(T.hl0[:, 128 * h:128 * h + 128], T.vh[:, h::2]))
+
+    P.wait_ge(T.sem.x1, n1)
+    w("P", e_pall, e_pt)
+    e_w8 = ev()
+    k = 0
+    for j, n in enumerate((2, 2, 2, 1, 1)):
+        bank = T["p%d" % (2 + j)]
+        e = ev()
+        for m in range(n):
+            inc(e, mm(bank[:, 128 * m:128 * m + 128], T.pall[:, k + m:k + m + 128], T.idb[:, :]))
+        qn = "VSVSV"[j]
+        if j in (0, 2):
+            h = j // 2
+            w("V", e_vl)
+            inc(e_hl, V.tensor_scalar(T.hl1[:, 128 * h:128 * h + 128], T.vl[:, h::2], 1.0, None, A.add))
+        w(qn, e)
+        inc(e_w8, copy(qn, T.win8[:, 128 * k:128 * (k + n)], bank[:, 0:128 * n]))
+        k += n
+    w("V", e_w8, e_w16)
+    w("S", e_w8, e_w16)
+    e_g = [ev(), ev()]
+    for h in range(2):
+        for half in range(2):
+            k = 2 * h + half
+            src = T.win8[:, :].indirect(T.w16[:, 64 * k:64 * k + 64])
+            inc(e_g[h], copy("VS"[half], T.gw[:, 1024 * k:1024 * k + 1024], src))
+    w("P", e_hl, e_lh, e_w8)
+    e_vp = ev()
+    for h in range(2):
+        for x in range(2):
+            out = T.p2[:, 256 * h + 128 * x:256 * h + 128 * x + 128]
+            mm(out, T["lh%d0" % x][:, :], T.hl0[:, 128 * h:128 * h + 128], True, False)
+            inc(e_vp, mm(out, T["lh%d1" % x][:, :], T.hl1[:, 128 * h:128 * h + 128], False, True))
+    w("S", e_vp)
+    e_vb = one(S.activation(T.vb[:, :], T.p2[:, :], Fn.Copy))
+    w("S", e_ml16, e_mn)
+    e_mv = one(S.activation(T.mv[:, :], T.mn[:, :].indirect(T.ml16[:, 0:32]), Fn.Copy))
+
+    w("P", e_qs, e_rt)
+    e_tt = ev()
+    for h in range(2):
+        bank = (T.p1, T.p6)[h]
+        w("P", e_g[h])
+        e = ev()
+        for p in range(16):
+            inc(e, mm(bank[:, 8 * p:8 * p + 8], T.gw[:, 2048 * h + p:2048 * h + 2048:16], T.qs[:, :]))
+        w("V", e, e_rt)
+        u, v = T["u%d" % h], T["v%d" % h]
+        e = one(V.tensor_tensor(u[:, :], bank[:, 0:128], T.rt[:, 128 * h:128 * h + 128], A.mult))
+        w("V", e)
+        e = one(V.tensor_scalar(v[:, :], u[:, :], 15, 1, A.logical_shift_right, A.bitwise_and))
+        w("V", e)
+        inc(e_tt, V.tensor_tensor(T.tt[:, 64 * h:64 * h + 64], v[:, 0::2], v[:, 1::2], A.max))
+    w("V", e_tt, e_msk)
+    e_ns = one(V.tensor_tensor_scan(T.sc[:, :], T.msk[:, :], T.tt[:, :], 0.0, A.mult, A.max))
+    ns = T.sc[:, 3:128:4]
+
+    w("V", e_ns, e_onesb)
+    e_cum = one(V.tensor_tensor_scan(T.cum[:, :], ns, T.onesb[:, 0:32], 0.0, A.add, A.subtract))
+    w("P", e_cum, e_tri)
+    e_base = one(mm(T.p0[:, 16:17], T.tri[:, :], T.cum[:, 31:32]))
+    w("V", e_xj)
+    e_e1 = one(V.tensor_tensor(T.e1[:, :], ns, T.xj[:, :], A.mult))
+    w("V", e_cum, e_e1)
+    e_e2 = one(V.tensor_tensor(T.e2[:, :], T.e1[:, :], T.cum[:, :], A.subtract))
+    w("V", e_base, e_e2)
+    e_off = one(V.tensor_scalar(T.off[:, :], T.e2[:, :], T.p0[:, 16:17], 1.0, A.subtract, A.subtract))
+    w("V", e_off, e_vb, e_win0)
+    e_sc = one(V.tensor_copy(T.win[:, 0:WIN].indirect(T.off[:, 0:32]), T.vb[:, :]))
+    w("P", e_sc, e_sel, e_ns)
+    e_ls = ev()
+    for b in range(4):
+        inc(e_ls, mm(T.p6[:, 128 + b:160:4], T.win[:, b:512:4], T.sel[:, :]))
+    w("V", e_ls)
+    e_z = one(V.tensor_copy(T.z16[:, :], T.p6[:, 128:160]))
+    e_own2 = one(V.tensor_copy(T.offo[:, 0:4], T.p6[:, 128 + 4 * me:132 + 4 * me]))
+
+    w("g", e_z)
+
+    def land2(r):
+        k = slot_of(r, me, T, topo)
+        return T.off2[:, 4 * k:4 * k + 4]
+    m2 = send(x2, lambda r: T.sem.x2, T.sem.l2, lambda r: T.z16[:, 4 * r:4 * r + 4], land2)
+
+    w("P", e_negb)
+    e_cnt = one(mm(T.p7[:, 128:129], T.negb[:, :], T.cum[:, 31:32]))
+    w("S", e_cnt)
+    e_yc = one(S.activation(T.yo[:, 64:65], T.p7[:, 128:129], Fn.Copy))
+    w("V", e_mv, e_mw0)
+    e_ms1 = one(V.tensor_copy(T.mwin[:, 0:WIN].indirect(T.off[:, 0:24]), T.mv[:, 0:384]))
+    window = T.at2[:, 0:16392]
+    w("S", e_own2, e_at)
+    S.wait_ge(T.sem.wn, nw)
+    e_own3 = one(copy("S", T.ga[:, 448:512], window.indirect(T.offo[:, 0:4])))
+
+    V.wait_ge(T.sem.wn, nw)
+    w("V", e_at)
+    e_ga = []
+    for qn in "VS":
+        names[qn].wait_ge(T.sem.x2, n2)
+    for qn, k, n in (("V", 0, 2), ("S", 2, 2), ("V", 4, 2), ("S", 6, 1)):
+        e_ga.append(one(copy(qn, T.ga[:, 64 * k:64 * (k + n)], window.indirect(T.off2[:, 4 * k:4 * (k + n)]))))
+
+    def land3(r):
+        k = slot_of(r, me, T, topo)
+        return T.rx3[:, 64 * k:64 * k + 64]
+
+    def sem3(r):
+        return (T.sem.x3a, T.sem.x3a, T.sem.x3b, T.sem.x3c)[slot_of(r, me, T, topo) // 2]
+
+    def block(r):
+        k = slot_of(me, r, T, topo)
+        return T.ga[:, 64 * k:64 * k + 64]
+    m3 = 0
+    for k, call in enumerate(x3):
+        w("g", e_ga[2 * k], e_ga[2 * k + 1])
+        m3 += send([call], sem3, T.sem.l3, block, land3)
+
+    w("V", e_ms1)
+    e_ms = one(V.tensor_copy(T.mwin[:, 0:WIN].indirect(T.off[:, 24:32]), T.mv[:, 384:512]))
+    w("P", e_ms, e_b7, e_w8)
+    for k in range(8):
+        e = mm(T.p5[:, 0:64], T.b7[:, 112 - 16 * k:240 - 16 * k], T.mwin[:, 64 * k:64 * k + 64], k == 0, k == 7)
+    e_mm = one(e)
+    w("V", e_mm, e_own3)
+    e_qm = ev()
+    for v in range(4):
+        inc(e_qm, V.tensor_tensor(T.qm[:, 16 * v:16 * v + 16], T.p5[:, v:64:4],
+                                  T.ga[:, 448 + 16 * v:464 + 16 * v], A.add))
+
+    V.wait_ge(T.sem.x3a, n3a)
+    e = one(V.tensor_tensor(T.q1[:, :], T.rx3[:, 0:128], T.rx3[:, 128:256], A.add))
+    w("V", e)
+    e = one(V.tensor_tensor(T.q2[:, :], T.q1[:, 0:64], T.q1[:, 64:128], A.add))
+    w("V", e, e_qm)
+    e = one(V.tensor_tensor(T.qf[:, :], T.q2[:, :], T.qm[:, :], A.add))
+    V.wait_ge(T.sem.x3c, n3c)
+    w("V", e)
+    e_qg = one(V.tensor_tensor(T.qg[:, :], T.qf[:, :], T.rx3[:, 384:448], A.add))
+    V.wait_ge(T.sem.x3b, n3b)
+    e = one(V.tensor_tensor(T.q3[:, :], T.rx3[:, 256:320], T.rx3[:, 320:384], A.add))
+    w("V", e, e_qg)
+    e_yo = ev()
+    for v in range(4):
+        inc(e_yo, V.tensor_tensor(T.yo[:, v:64:4], T.q3[:, 16 * v:16 * v + 16], T.qg[:, 16 * v:16 * v + 16], A.add))
+    e_y = ev()
+    for k in range(8):
+        qn = "YS"[k % 2]
+        n = 65 if k == 7 else 64
+        w(qn, e_yo, e_yc)
+        inc(e_y, names[qn].dma_start(T.y[:, 64 * k:64 * k + n], T.yo[16 * k:16 * k + 16, 0:n]), 16)
+    g.wait_ge(T.sem.l0, m0)
+    g.wait_ge(T.sem.l1, m1)
+    g.wait_ge(T.sem.l2, m2)
+    g.wait_ge(T.sem.l3, m3)
+    w("g", e_y)
+    for e in range(len(evs)):
+        if e not in waited:
+            w("g", e)

@@ -5,37 +5,46 @@ from concourse.mybir import AluOpType as A, ActivationFunctionType as Fn
 F32, BF, I32, U16 = "float32", "bfloat16", "int32", "uint16"
 WIN = 5120
 ROWS = 16384
-PARTS = (1920, 1792, 1792)
-OWN = ROWS - sum(PARTS)
+PAD = 96
+NV = 20
+CHUNK = ((640, 640, 640), (1152, 1152, 1152))
+OWN = ROWS - sum(map(sum, CHUNK))
+EARLY = 1024
+LN2 = math.log(2.0)
 SCRATCH = {}
 for _t, _list in (
-        (BF, "f1 128,f2 128,pall 136,onesb 128,negb 128,m16 16,wp 16,idb 128,tri 128,qs0 8,qs 8,"
-             "bb 256,rb 256,vb 512,win8 1024,gw 4096,tt 128,sc 128,msk 128,cum 32,win 5120,sel 8,selh 8,"
-             "lh00 128,lh01 128,lh10 128,lh11 128,hl0 256,hl1 256"),
-        (I32, "a0 128,im 16,im2 16,im8 8,gi 1,fks 256,wi 256,bi 256,u0 128,u1 128,v0 128,v1 128,mn 512,"
-              "ml 32,ml2 32,at2 16392,vr 256,vh 256,vl 256,hw 1920"),
-        (F32, "onesf 128,m8f 8,gf 1,gpf 1,xj 32,rt 256,e1 32,e2 32,ga 512,rx3 448,q1 128,q2 64,q3 64,qm 64,qf 64,qg 64,"
-              "mv 512,mwin 5120,b7 240,yo 68"),
-        (U16, "w16 256,off 32,off2 32,offo 8,ml16 32,z16 32")):
+        (BF, "f1 128,f2 128,pall 136,onesb 128,negb 128,wp 16,we 16,wm 16,idb 128,tri 128,qs0 8,qs 8,"
+             "bb 256,rb 256,win8 1024,gw 4096,tt 128,sc 128,msk 128,cum 32,vb 512,win 5120,sel 8,pm 128,"
+             "lh0 128,lh1 128,hb 256,qt 32"),
+        (I32, "a0 128,im 16,im2 16,iv 16,iv2 16,fks 256,wi 256,u0 128,u1 128,v0 128,v1 128,mn 512,"
+              "ml 32,ml2 32,at2 16480,vr 256,od 1"),
+        (F32, "onesf 128,ivf 16,xj 32,rt 256,e1 32,e2 32,ga 512,rx3 448,qm 64,kf 256,lk0 128,lk1 128,"
+              "mv 512,vbf 512,win2 5120,mwin 5120,b7 240,yo 64,yc 2,prm 128,m16 16,self 8,bz 1"),
+        (U16, "w16 256,off 32,off2 32,ml16 32,z16 32")):
     for _x in _list.split(","):
         SCRATCH[_x.split()[0]] = ("sbuf", [128, int(_x.split()[1])], _t)
-for _k in range(3):
-    SCRATCH["hd%d" % _k] = ("dram", [2, 128, PARTS[_k] // 16], I32)
-    SCRATCH["raw%d" % _k] = ("sbuf", [128, PARTS[_k] // 8], I32)
+for _t in range(2):
+    for _i in range(3):
+        SCRATCH["hd%d%d" % (_t, _i)] = ("dram", [128, CHUNK[_t][_i] // 8], I32)
+        SCRATCH["raw%d%d" % (_t, _i)] = ("dram", [128, CHUNK[_t][_i] // 8], I32)
+for _t in range(2):
+    SCRATCH["hw%d" % _t] = ("sbuf", [128, max(CHUNK[_t])], I32)
 SCRATCH["lm"] = ("sbuf", [1, 2], I32)
 SCRATCH["lf"] = ("sbuf", [1, 2], F32)
-for _k in range(8):
+for _k in range(4):
     SCRATCH["p%d" % _k] = ("psum", [128, 512], F32)
-SEMAPHORES = ["x1", "x2", "x3a", "x3b", "x3c", "l0", "l1", "l2", "l3", "hr", "wn"] + ["e%d" % k for k in range(130)]
+    SCRATCH["t%d" % _k] = ("psum", [128, 1024], BF)
+SEMAPHORES = ["x1", "x2a", "x2b", "x2c", "x2d", "x3a", "x3b", "x3c", "x3d", "l0", "l1", "l2", "l3", "hr0", "hr1", "wn", "go"] + [
+    "e%d" % k for k in range(130)]
 
 
 def helpers(core, T, topo):
     hs = [c for c in topo.cores_of(core) if c not in T.cores and topo.die(c) == topo.die(core)]
-    return hs[:len(PARTS)]
+    return hs[:3]
 
 
-def part_start(i, t=0):
-    return 1 + OWN + sum(PARTS[:i]) + t * PARTS[i] // 2
+def chunk_start(t, i):
+    return OWN + sum(sum(c) for c in CHUNK[:t]) + sum(CHUNK[t][:i])
 
 
 def distance_order(core, T, topo):
@@ -70,11 +79,6 @@ def engine_sets(core, T, topo):
     return eo, [e for e in topo.engines(core, T.cores[near[0]]) if e not in eo]
 
 
-def helper_engines(core, T, topo):
-    eo, en = engine_sets(core, T, topo)
-    return [[eo, en], [eo[:4], eo[4:]], [en[:4], en[4:]]]
-
-
 def plans(core, T, topo):
     me = T.rank_of(core)
     order = distance_order(core, T, topo)
@@ -82,11 +86,9 @@ def plans(core, T, topo):
     near = [r for r in order[-1][1] if r != me]
     eo, en = engine_sets(core, T, topo)
     x1 = [[(far, eo), (near, en[:2])]]
-    x2 = [[([far[k]], eo[2 * k:2 * k + 2]) for k in range(4)] + [(near, en[:2])],
-          [([far[4 + k]], eo[4 * k:4 * k + 4]) for k in range(2)]]
-    x3 = [[([far[k]], eo[2 * k:2 * k + 2]) for k in range(4)],
-          [([far[4 + k]], eo[4 * k:4 * k + 4]) for k in range(2)] + [(near, en[:4])]]
-    return order, x1, x2, x3
+    x2 = [[([far[2 * j + k]], eo[4 * k:4 * k + 4]) for k in range(2)] for j in range(3)]
+    x2[1].append((near, en[:4]))
+    return order, x1, x2, x2
 
 
 def arriving(core, T, topo, which, slots=range(8)):
@@ -109,24 +111,35 @@ def transfer(dest_cores, eng, rsem, src, dst, topo):
                              dsts=[dst] * len(ids))
 
 
+RAW_CALLS = (((0, 0), (0, 1), (0, 2)), ((1, 0), (1, 1), (1, 2)))
+
+
+def raw_engines(owner, helper, t, i, topo):
+    eng = topo.engines(owner, helper)
+    call = [c for c in RAW_CALLS if (t, i) in c][0]
+    n = len(eng) >> (len(call) - 1).bit_length()
+    k = call.index((t, i))
+    return eng[n * k:n * k + n]
+
+
 def helper_program(g, core, T, topo):
     owners = [c for c in T.cores if core in helpers(c, T, topo)]
     if not owners:
         return
     owner = owners[0]
     i = helpers(owner, T, topo).index(core)
-    n = PARTS[i] // 2
-    for q in (g.sync, g.scalar):
-        q.wait_ge(T.sem.hr, sum(len(e) for e in helper_engines(owner, T, topo)[i]))
     for t in range(2):
+        n = CHUNK[t][i]
+        for q in (g.sync, g.scalar):
+            q.wait_ge(T.sem["hr%d" % t], len(raw_engines(owner, core, t, i, topo)))
         for k in range(8):
             q = (g.sync, g.scalar)[k % 2]
-            q.dma_start(T.hw[16 * k:16 * k + 16, n * t:n * t + n], T["hd%d" % i][t]).then_inc(T.sem["e%d" % t], 16)
+            q.dma_start(T["hw%d" % t][16 * k:16 * k + 16, 0:n], T["hd%d%d" % (t, i)][:, :]).then_inc(T.sem["e%d" % t], 16)
     eng = topo.engines(core, owner)
     for t in range(2):
         g.wait_ge(T.sem["e%d" % t], 128)
-        c0 = part_start(i, t)
-        g.remote_dma_fused([transfer([owner], eng, T.sem.wn, T.hw[:, n * t:n * t + n], T.at2[:, c0:c0 + n], topo)],
+        c0, n = PAD + chunk_start(t, i), CHUNK[t][i]
+        g.remote_dma_fused([transfer([owner], eng, T.sem.wn, T["hw%d" % t][:, 0:n], T.at2[:, c0:c0 + n], topo)],
                            local_sem=T.sem.l0)
     g.wait_ge(T.sem.l0, 2 * len(eng))
 
@@ -168,11 +181,12 @@ def rank_program(g, core, T, topo):
         return V.tensor_copy(out, in_) if qn == "V" else S.activation(out, in_, Fn.Copy)
 
     order, x1, x2, x3 = plans(core, T, topo)
-    n1, n2 = arriving(core, T, topo, 1), arriving(core, T, topo, 2)
-    n3a, n3b, n3c = [arriving(core, T, topo, 3, s) for s in (range(4), range(4, 6), range(6, 8))]
-    hs, heng = helpers(core, T, topo), helper_engines(core, T, topo)
+    n1 = arriving(core, T, topo, 1)
+    n2 = [arriving(core, T, topo, 2, range(2 * k, 2 * k + 2)) for k in range(4)]
+    n3 = [arriving(core, T, topo, 3, range(2 * k, 2 * k + 2)) for k in range(4)]
+    hs = helpers(core, T, topo)
     nw = sum(2 * len(topo.engines(h, core)) for h in hs)
-    m0 = sum(len(e) for h in heng for e in h)
+    m0 = 0
 
     def send(calls, rsem, lsem, src, dst):
         n = 0
@@ -182,159 +196,160 @@ def rank_program(g, core, T, topo):
             n += sum(len(eng) for dests, eng in call)
         return n
 
-    def raw(i, t):
-        n = PARTS[i] // 16
-        return T["raw%d" % i][:, n * t:n * t + n]
+    def send_raw(call):
+        engs = [raw_engines(core, hs[i], t, i, topo) for t, i in call]
+        g.remote_dma_fused([transfer([hs[i]], eng, T.sem["hr%d" % t], T["raw%d%d" % (t, i)][:, :],
+                                     T["hd%d%d" % (t, i)][:, :], topo) for (t, i), eng in zip(call, engs)],
+                           local_sem=T.sem.l0)
+        return sum(map(len, engs))
 
-    def send_raw(which):
-        g.remote_dma_fused([transfer([hs[i]], heng[i][t], T.sem.hr, raw(i, t), T["hd%d" % i][t], topo)
-                            for i in which for t in range(2)], local_sem=T.sem.l0)
-
-    def raw_load(q, i):
+    def raw_load(queues, call):
         e = ev()
-        for t in range(2):
-            c0 = part_start(i, t) - 1
-            inc(e, q.dma_start(raw(i, t), T["at"][:, c0:c0 + PARTS[i] // 2]), 16)
+        for k, (t, i) in enumerate(call):
+            c0 = chunk_start(t, i)
+            inc(e, queues[k % len(queues)].dma_start(T["raw%d%d" % (t, i)][:, :], T["at"][:, c0:c0 + CHUNK[t][i]]), 16)
         return e
+
+    def own_load(e, c0, c1, groups):
+        for k in groups:
+            inc(e, Y.dma_start(T.at2[16 * k:16 * k + 16, PAD + c0:PAD + c1], T["at"][:, c0:c1]), 16)
 
     e_lim = one(S.dma_start(T.lm[:, :], T.lim[:, :]), 16)
     e_a0 = one(Y.dma_start(T.a0[:, :], T["at"][0:1, :]), 16)
-    e_fk = one(S.dma_start(T.fks[:, :], T.fk[:, :]), 16)
-    e_raw = [raw_load(Y, 0)]
+    e_raw = [raw_load((S, Y), RAW_CALLS[0])]
+    e_fk = one(Y.dma_start(T.fks[:, :], T.fk[:, :]), 16)
+    e_mn0 = one(V.memset(T.mn[:, :], 0))
+    w("Y", e_mn0)
+    e_mn = one(Y.dma_start(T.mn[0::16, :], T["me"][0:1, :]), 16)
     e_vr = ev()
     for k in range(8):
         inc(e_vr, Y.dma_start(T.vr[16 * k:16 * k + 16, :], T.fk[:, 32 * k:32 * k + 32]), 16)
-    e_raw += [raw_load(Y, 1), raw_load(Y, 2)]
+    e_raw += [raw_load((Y,), call) for call in RAW_CALLS[1:]]
 
+    e_ivf = one(g.iota(T.ivf[:, :], [[-64, 2], [-1, 8]], 0, 1, allow_small_or_imprecise_dtypes=True))
+    e_iv = one(g.iota(T.iv[:, :], [[-64, 2], [-1, 8]], 0, 1))
     e_im = one(g.iota(T.im[:, :], [[-1, 16]], 0, 1))
     e_ml = one(g.iota(T.ml[:, :], [[1, 32]], 0, 32))
     e_onesb = one(V.memset(T.onesb[:, :], 1.0))
     e_onesf = one(V.memset(T.onesf[:, :], 1.0))
+    e_pt = one(V.memset(T.pall[:, 128:136], 0.0))
+    w("S", e_ivf)
+    e_we = one(S.activation(T.we[:, :], T.ivf[:, :], Fn.Exp, scale=LN2 / 8))
+    w("V", e_iv)
+    e_iv2 = one(V.tensor_scalar(T.iv2[:, :], T.iv[:, :], 0x7FFFFFC7, None, A.bitwise_and))
     w("V", e_im)
-    e_gi = one(V.tensor_scalar(T.gi[:, :], T.im[:, 0:1], 3, 7, A.logical_shift_right, A.bitwise_and))
-    e_im8 = one(V.tensor_scalar(T.im8[:, :], T.im[:, 0:8], 7, None, A.bitwise_and))
-    w("V", e_gi)
-    e_gf = one(V.tensor_copy(T.gf[:, :], T.gi[:, :]))
-    w("S", e_gf)
-    e_gp = one(S.activation(T.gpf[:, :], T.gf[:, :], Fn.Exp, scale=math.log(2.0)))
     e_im2 = one(V.tensor_scalar(T.im2[:, :], T.im[:, :], 15, None, A.bitwise_and))
-    w("V", e_im8)
-    e_m8f = one(V.tensor_scalar(T.m8f[:, :], T.im8[:, :], 0.0, None, A.is_equal))
-    e_wp = one(V.memset(T.wp[:, :], 0.0))
-    w("V", e_im2)
-    e_m16 = one(V.tensor_scalar(T.m16[:, :], T.im2[:, :], 0.0, None, A.is_equal))
+    e_slot = one(V.memset(T.at2[:, 0:PAD], 0))
+    e_od = one(V.tensor_scalar(T.od[:, :], T.im[:, 0:1], 1, None, A.bitwise_and))
+    e_qt = one(V.memset(T.qt[:, :], 0.25))
+    w("V", e_iv2)
+    e_wm = one(V.tensor_scalar(T.wm[:, :], T.iv2[:, :], 0.0, None, A.is_equal))
     w("V", e_ml)
     e_ml2 = one(V.tensor_scalar(T.ml2[:, :], T.ml[:, :], 511, None, A.bitwise_and))
-    e_pt = one(V.memset(T.pall[:, 128:136], 0.0))
-    w("V", e_m16)
-    e_selh = one(V.tensor_scalar(T.selh[:, :], T.m16[:, 0::2], 128.0, None, A.mult))
+    w("V", e_im2)
+    e_m16 = one(V.tensor_scalar(T.m16[:, :], T.im2[:, :], 0.0, None, A.is_equal))
     w("V", e_ml2)
     e_ml16 = one(V.tensor_copy(T.ml16[:, :], T.ml2[:, :]))
-    w("V", e_selh)
-    e_sel = one(V.tensor_tensor(T.sel[:, :], T.selh[:, :], T.m16[:, 1::2], A.add))
-    e_slot = one(V.memset(T.at2[:, 0:1], 0))
+    w("V", e_od, e_m16)
+    e_bz = one(V.tensor_scalar(T.bz[:, :], T.od[:, :], 64.0, None, A.mult))
+    e_sel = ev()
+    for t in (T.sel, T["self"]):
+        inc(e_sel, V.tensor_tensor(t[:, :], T.m16[:, 0::2], T.m16[:, 1::2], A.add))
+    w("V", e_wm, e_we)
+    e_w = one(V.tensor_tensor(T.wp[:, :], T.we[:, :], T.wm[:, :], A.mult))
     w("g", e_onesb)
     e_id = one(g.affine_select(T.idb[:, :], T.onesb[:, :], [[-1, 128]], A.is_equal, 0.0, 0, 1))
-    e_tri = one(g.affine_select(T.tri[:, :], T.onesb[:, :], [[1, 128]], A.is_gt, 0.0, 0, -1))
+    e_pm = one(g.iota(T.pm[:, :], [[0, 64], [-2, 2]], 1, 0, allow_small_or_imprecise_dtypes=True))
+    w("S", e_onesf)
+    e_win0 = ev()
+    for k in range(4):
+        inc(e_win0, S.activation(T.win[:, 128 * k:128 * k + 128], T.onesf[:, :], Fn.Copy, scale=0.0))
+    w("S", e_ml16, e_mn)
+    e_mv = one(S.activation(T.mv[:, :], T.mn[:, :].indirect(T.ml16[:, 0:32]), Fn.Copy))
 
     w("g", e_raw[0])
-    send_raw([0])
+    m0 += send_raw(RAW_CALLS[0])
 
     w("V", e_lim)
     e_lf = one(V.tensor_copy(T.lf[:, :], T.lm[:, :]))
     w("P", e_lf, e_onesf)
     e_lp = one(mm(T.p0[:, 0:2], T.onesf[0:1, :], T.lf[:, :]))
-    w("V", e_wp, e_m8f, e_gp)
-    e_w = ev()
-    for x in range(2):
-        s = slice(64 * x, 64 * x + 64)
-        inc(e_w, V.tensor_scalar(T.wp[s, 8 * x:8 * x + 8], T.m8f[s, :], T.gpf[s, 0:1], None, A.mult))
     w("V", e_lp, e_a0)
     e_f1 = one(V.tensor_scalar(T.f1[:, :], T.a0[:, :], T.p0[:, 0:1], None, A.is_lt))
     e_f2 = one(V.tensor_scalar(T.f2[:, :], T.a0[:, :], T.p0[:, 1:2], None, A.is_gt))
+    w("V", e_fk)
+    e_bb = one(V.tensor_scalar(T.bb[:, :], T.fks[:, :], 163840.0 - 511.5, None, A.add))
     w("P", e_w, e_f1)
-    mm(T.p7[:, 0:16], T.f1[:, :], T.wp[:, :], True, False)
+    mm(T.p3[:, 0:16], T.f1[:, :], T.wp[:, :], True, False)
     w("P", e_f2)
-    e_pk = one(mm(T.p7[:, 0:16], T.f2[:, :], T.wp[:, :], False, True))
+    e_pk = one(mm(T.p3[:, 0:16], T.f2[:, :], T.wp[:, :], False, True))
     w("V", e_pk)
     slot1 = T.pall[:, 16 * me:16 * me + 16]
-    e_pall = one(V.tensor_copy(slot1, T.p7[:, 0:16]))
+    e_pall = one(V.tensor_copy(slot1, T.p3[:, 0:16]))
 
     w("g", e_pall)
     m1 = send(x1, lambda r: T.sem.x1, T.sem.l1, lambda r: slot1, lambda r: slot1)
-    w("g", e_raw[1], e_raw[2])
-    send_raw([1, 2])
+    g.sem_inc(T.sem.go, 1)
+    for k in range(1, len(RAW_CALLS)):
+        w("g", e_raw[k])
+        m0 += send_raw(RAW_CALLS[k])
 
-    e_mn0 = one(g.iota(T.mn[:, :], [[0, 512]], 0, 0))
+    w("Y", e_slot)
+    e_at = ev()
+    if EARLY:
+        own_load(e_at, 0, EARLY, range(8))
+    Y.wait_ge(T.sem.go, 1)
+    own_load(e_at, EARLY, OWN, range(8))
+
+    e_lh = ev()
+    w("g", e_pm, e_onesf)
+    for x in range(2):
+        inc(e_lh, g.affine_select(T["lh%d" % x][:, :], T.pm[:, :], [[-2, 64], [0, 2]], A.is_equal, 0.0, -x, 1))
+        inc(e_lh, g.affine_select(T["lk%d" % x][:, :], T.onesf[:, :], [[-2, 64], [1000, 2]], A.is_equal, 0.0,
+                                  -x - 1000, 1))
     e_qs0 = one(g.affine_select(T.qs0[:, :], T.onesb[:, 0:8], [[-16, 8]], A.is_equal, 0.0, 0, 1))
     w("g", e_qs0)
     e_qs = one(g.affine_select(T.qs[:, :], T.qs0[:, :], [[-16, 8]], A.not_equal, 256.0, -8, 1))
-    e_lh = ev()
-    for x in range(2):
-        for hl in range(2):
-            inc(e_lh, g.affine_select(T["lh%d%d" % (x, hl)][:, :], T.onesb[:, :], [[-2, 64], [1000, 2]], A.is_equal, 0.0,
-                                      -x - 1000 * hl, 1))
     e_msk = one(g.affine_select(T.msk[:, :], T.onesb[:, :], [[0, 32], [1, 4]], A.not_equal, 0.0, 0, 0))
+    e_tri = one(g.affine_select(T.tri[:, :], T.onesb[:, :], [[1, 128]], A.is_gt, 0.0, 0, -1))
     e_xj = one(g.iota(T.xj[:, :], [[1, 32]], 513, 32, allow_small_or_imprecise_dtypes=True))
-    e_win0 = one(g.iota(T.win[:, 0:512], [[0, 512]], 0, 0, allow_small_or_imprecise_dtypes=True))
-    e_mw0 = one(g.iota(T.mwin[:, 0:512], [[0, 512]], 0, 0, allow_small_or_imprecise_dtypes=True))
     e_negb = one(g.iota(T.negb[:, :], [[0, 128]], -1, 0, allow_small_or_imprecise_dtypes=True))
     e_b70 = one(g.iota(T.b7[:, :], [[0, 240]], 1, 0, allow_small_or_imprecise_dtypes=True))
     w("g", e_b70)
     e_b7 = one(g.affine_select(T.b7[:, :], T.b7[:, :], [[1, 15], [0, 16]], A.is_equal, 0.0, -7, 0))
+    e_perm = one(g.affine_select(T.prm[:, :], T.onesf[:, :], [[-1, 16], [-16, 8]], A.is_equal, 0.0, 0, 1))
 
-    w("Y", e_slot)
-    Y.wait_ge(T.sem.l1, m1)
-    e_at = ev()
-    for k in range(8):
-        inc(e_at, Y.dma_start(T.at2[16 * k:16 * k + 16, 1:OWN + 1], T["at"][:, 0:OWN]), 16)
-        if k == 3:
-            w("Y", e_mn0)
-            e_mn = one(Y.dma_start(T.mn[0::16, :], T["me"][0:1, :]), 16)
-
-    w("V", e_fk)
-    e_bi = one(V.tensor_scalar(T.bi[:, :], T.fks[:, :], 10, None, A.arith_shift_right))
     e_wi = one(V.tensor_scalar(T.wi[:, :], T.fks[:, :], 1023, None, A.bitwise_and))
-    w("V", e_bi)
-    e_bb = ev()
-    for h in range(2):
-        inc(e_bb, V.tensor_copy(T.bb[:, 128 * h:128 * h + 128], T.bi[:, h::2]))
     w("V", e_wi)
     e_w16 = ev()
     for h in range(2):
         inc(e_w16, V.tensor_copy(T.w16[:, 128 * h:128 * h + 128], T.wi[:, h::2]))
     w("S", e_bb)
-    e_rb = one(S.activation(T.rb[:, :], T.bb[:, :], Fn.Exp, scale=-math.log(2.0)))
+    e_rb = one(S.activation(T.rb[:, :], T.bb[:, :], Fn.Exp, bias=175 * LN2, scale=-LN2 / 1024))
+    e_win20 = ev()
+    for k in range(4):
+        inc(e_win20, S.activation(T.win2[:, 128 * k:128 * k + 128], T.onesf[:, :], Fn.Silu, scale=0.0))
     w("P", e_rb, e_id)
     e_rp = ev()
     for h in range(2):
         for d in range(8):
-            inc(e_rp, mm(T.p1[:, 128 * h + d:128 * h + 128:8], T.rb[:, 128 * h:128 * h + 128],
-                         T.idb[:, 16 * d:16 * d + 16]))
-    w("S", e_rp)
-    e_rt = one(S.activation(T.rt[:, :], T.p1[:, 0:256], Fn.Copy, scale=32768.0))
+            inc(e_rp, mm(T.p1[:, 128 * h + d:128 * h + 128:8], T.rb[:, h::2], T.idb[:, 16 * d:16 * d + 16]))
     w("V", e_vr)
-    e_vh = one(V.tensor_scalar(T.vh[:, :], T.vr[:, :], 7, None, A.arith_shift_right))
-    e_vl = one(V.tensor_scalar(T.vl[:, :], T.vr[:, :], 127, None, A.bitwise_and))
-    e_hl = ev()
-    w("V", e_vh)
-    for h in range(2):
-        inc(e_hl, V.tensor_copy(T.hl0[:, 128 * h:128 * h + 128], T.vh[:, h::2]))
+    e_kf = ev()
+    for t in (T.kf, T.hb):
+        inc(e_kf, V.tensor_scalar(t[:, :], T.vr[:, :], 32.0, None, A.add))
+    w("V", e_rp)
+    e_rt = one(V.tensor_copy(T.rt[:, :], T.p1[:, 0:256]))
 
     P.wait_ge(T.sem.x1, n1)
     w("P", e_pall, e_pt)
     e_w8 = ev()
     k = 0
-    for j, n in enumerate((2, 2, 2, 1, 1)):
-        bank = T["p%d" % (2 + j)]
+    for j, (qn, n) in enumerate((("S", 2), ("V", 3), ("S", 1), ("V", 2))):
+        bank = T["t%d" % j]
         e = ev()
         for m in range(n):
-            inc(e, mm(bank[:, 128 * m:128 * m + 128], T.pall[:, k + m:k + m + 128], T.idb[:, :]))
-        qn = "VSVSV"[j]
-        if j in (0, 2):
-            h = j // 2
-            w("V", e_vl)
-            inc(e_hl, V.tensor_scalar(T.hl1[:, 128 * h:128 * h + 128], T.vl[:, h::2], 1.0, None, A.add))
+            inc(e, P.transpose(bank[:, 128 * m:128 * m + 128], T.pall[:, k + m:k + m + 128], T.idb[:, :]))
         w(qn, e)
         inc(e_w8, copy(qn, T.win8[:, 128 * k:128 * (k + n)], bank[:, 0:128 * n]))
         k += n
@@ -346,22 +361,24 @@ def rank_program(g, core, T, topo):
             k = 2 * h + half
             src = T.win8[:, :].indirect(T.w16[:, 64 * k:64 * k + 64])
             inc(e_g[h], copy("VS"[half], T.gw[:, 1024 * k:1024 * k + 1024], src))
-    w("P", e_hl, e_lh, e_w8)
+    w("P", e_kf, e_lh)
     e_vp = ev()
     for h in range(2):
         for x in range(2):
             out = T.p2[:, 256 * h + 128 * x:256 * h + 128 * x + 128]
-            mm(out, T["lh%d0" % x][:, :], T.hl0[:, 128 * h:128 * h + 128], True, False)
-            inc(e_vp, mm(out, T["lh%d1" % x][:, :], T.hl1[:, 128 * h:128 * h + 128], False, True))
-    w("S", e_vp)
-    e_vb = one(S.activation(T.vb[:, :], T.p2[:, :], Fn.Copy))
-    w("S", e_ml16, e_mn)
-    e_mv = one(S.activation(T.mv[:, :], T.mn[:, :].indirect(T.ml16[:, 0:32]), Fn.Copy))
+            mm(out, T["lh%d" % x][:, :], T.hb[:, h::2], True, False)
+            inc(e_vp, mm(out, T["lk%d" % x][:, :], T.kf[:, h::2], False, True))
+    w("S", e_vp, e_bz)
+    e_vb = one(S.activation(T.vb[:, 0:16 * NV], T.p2[:, 0:16 * NV], Fn.Identity, bias=T.bz[:, 0:1]))
+    e_vbf = one(S.activation(T.vbf[:, 16 * NV:512], T.p2[:, 16 * NV:512], Fn.Identity, bias=T.bz[:, 0:1]))
+    e_mw0 = ev()
+    for k in range(4):
+        inc(e_mw0, S.activation(T.mwin[:, 128 * k:128 * k + 128], T.onesf[:, :], Fn.Copy, scale=0.0))
 
-    w("P", e_qs, e_rt)
+    w("P", e_qs, e_rt, e_pall)
     e_tt = ev()
     for h in range(2):
-        bank = (T.p1, T.p6)[h]
+        bank = (T.p1, T.p3)[h]
         w("P", e_g[h])
         e = ev()
         for p in range(16):
@@ -387,90 +404,92 @@ def rank_program(g, core, T, topo):
     e_e2 = one(V.tensor_tensor(T.e2[:, :], T.e1[:, :], T.cum[:, :], A.subtract))
     w("V", e_base, e_e2)
     e_off = one(V.tensor_scalar(T.off[:, :], T.e2[:, :], T.p0[:, 16:17], 1.0, A.subtract, A.subtract))
+    w("P", e_off, e_negb)
+    e_cnt = one(mm(T.p0[:, 32:34], T.negb[:, :], T.cum[:, 30:32]))
     w("V", e_off, e_vb, e_win0)
-    e_sc = one(V.tensor_copy(T.win[:, 0:WIN].indirect(T.off[:, 0:32]), T.vb[:, :]))
-    w("P", e_sc, e_sel, e_ns)
-    e_ls = ev()
-    for b in range(4):
-        inc(e_ls, mm(T.p6[:, 128 + b:160:4], T.win[:, b:512:4], T.sel[:, :]))
+    e_sc = one(V.tensor_copy(T.win[:, 0:WIN].indirect(T.off[:, 0:NV]), T.vb[:, 0:16 * NV]))
+    w("S", e_off, e_vbf, e_win20)
+    e_sc2 = one(S.activation(T.win2[:, 0:WIN].indirect(T.off[:, NV:32]), T.vbf[:, 16 * NV:512], Fn.Silu))
+    w("P", e_qt, e_sel)
+    mm(T.p3[:, 128:160], T.onesb[0:1, :], T.qt[0:1, :], True, False)
+    for e, win, sel in ((e_sc2, T.win2, T["self"]), (e_sc, T.win, T.sel)):
+        w("P", e)
+        for b in range(4):
+            last = mm(T.p3[:, 128 + b:160:4], win[:, b:512:4], sel[:, :], False, e == e_sc and b == 3)
+    e_ls = one(last)
     w("V", e_ls)
-    e_z = one(V.tensor_copy(T.z16[:, :], T.p6[:, 128:160]))
-    e_own2 = one(V.tensor_copy(T.offo[:, 0:4], T.p6[:, 128 + 4 * me:132 + 4 * me]))
+    e_z = one(V.tensor_copy(T.z16[:, :], T.p3[:, 128:160]))
 
     w("g", e_z)
 
     def land2(r):
         k = slot_of(r, me, T, topo)
         return T.off2[:, 4 * k:4 * k + 4]
-    m2 = send(x2, lambda r: T.sem.x2, T.sem.l2, lambda r: T.z16[:, 4 * r:4 * r + 4], land2)
 
-    w("P", e_negb)
-    e_cnt = one(mm(T.p7[:, 128:129], T.negb[:, :], T.cum[:, 31:32]))
-    w("S", e_cnt)
-    e_yc = one(S.activation(T.yo[:, 64:65], T.p7[:, 128:129], Fn.Copy))
+    def sem2(r):
+        return T.sem["x2" + "abcd"[slot_of(r, me, T, topo) // 2]]
+    m2 = send(x2, sem2, T.sem.l2, lambda r: T.z16[:, 4 * r:4 * r + 4], land2)
+
+    w("V", e_cnt)
+    e_yc = one(V.tensor_copy(T.yc[:, :], T.p0[:, 32:34]))
+    w("Y", e_yc)
+    e_y0 = one(Y.dma_start(T.y[:, 511:513], T.yc[0:16, :]), 16)
     w("V", e_mv, e_mw0)
-    e_ms1 = one(V.tensor_copy(T.mwin[:, 0:WIN].indirect(T.off[:, 0:24]), T.mv[:, 0:384]))
-    window = T.at2[:, 0:16392]
-    w("S", e_own2, e_at)
+    e_ms1 = one(V.tensor_copy(T.mwin[:, 0:WIN].indirect(T.off[:, 0:16]), T.mv[:, 0:256]))
+    window = T.at2[:, :]
+    w("S", e_z, e_at)
     S.wait_ge(T.sem.wn, nw)
-    e_own3 = one(copy("S", T.ga[:, 448:512], window.indirect(T.offo[:, 0:4])))
+    e_own3 = one(copy("S", T.ga[:, 448:512], window.indirect(T.z16[:, 4 * me:4 * me + 4])))
 
     V.wait_ge(T.sem.wn, nw)
     w("V", e_at)
-    e_ga = []
-    for qn in "VS":
-        names[qn].wait_ge(T.sem.x2, n2)
-    for qn, k, n in (("V", 0, 2), ("S", 2, 2), ("V", 4, 2), ("S", 6, 1)):
-        e_ga.append(one(copy(qn, T.ga[:, 64 * k:64 * (k + n)], window.indirect(T.off2[:, 4 * k:4 * (k + n)]))))
+    e_ga = [ev() for call in x3]
+    for j, qn, k in ((0, "V", 0), (0, "S", 1), (1, "V", 2), (1, "S", 3), (1, "S", 6), (2, "V", 4), (2, "S", 5)):
+        names[qn].wait_ge(T.sem["x2" + "abcd"[k // 2]], n2[k // 2])
+        inc(e_ga[j], copy(qn, T.ga[:, 64 * k:64 * k + 64], window.indirect(T.off2[:, 4 * k:4 * k + 4])))
 
     def land3(r):
         k = slot_of(r, me, T, topo)
         return T.rx3[:, 64 * k:64 * k + 64]
 
     def sem3(r):
-        return (T.sem.x3a, T.sem.x3a, T.sem.x3b, T.sem.x3c)[slot_of(r, me, T, topo) // 2]
+        return T.sem["x3" + "abcd"[slot_of(r, me, T, topo) // 2]]
 
     def block(r):
         k = slot_of(me, r, T, topo)
         return T.ga[:, 64 * k:64 * k + 64]
     m3 = 0
     for k, call in enumerate(x3):
-        w("g", e_ga[2 * k], e_ga[2 * k + 1])
+        w("g", e_ga[k])
         m3 += send([call], sem3, T.sem.l3, block, land3)
 
     w("V", e_ms1)
-    e_ms = one(V.tensor_copy(T.mwin[:, 0:WIN].indirect(T.off[:, 24:32]), T.mv[:, 384:512]))
-    w("P", e_ms, e_b7, e_w8)
+    e_ms = one(V.tensor_copy(T.mwin[:, 0:WIN].indirect(T.off[:, 16:32]), T.mv[:, 256:512]))
+    w("P", e_ms, e_b7)
     for k in range(8):
-        e = mm(T.p5[:, 0:64], T.b7[:, 112 - 16 * k:240 - 16 * k], T.mwin[:, 64 * k:64 * k + 64], k == 0, k == 7)
+        e = mm(T.p1[:, 0:64], T.b7[:, 112 - 16 * k:240 - 16 * k], T.mwin[:, 64 * k:64 * k + 64], k == 0, k == 7)
     e_mm = one(e)
     w("V", e_mm, e_own3)
     e_qm = ev()
     for v in range(4):
-        inc(e_qm, V.tensor_tensor(T.qm[:, 16 * v:16 * v + 16], T.p5[:, v:64:4],
+        inc(e_qm, V.tensor_tensor(T.qm[:, 16 * v:16 * v + 16], T.p1[:, v:64:4],
                                   T.ga[:, 448 + 16 * v:464 + 16 * v], A.add))
 
-    V.wait_ge(T.sem.x3a, n3a)
-    e = one(V.tensor_tensor(T.q1[:, :], T.rx3[:, 0:128], T.rx3[:, 128:256], A.add))
-    w("V", e)
-    e = one(V.tensor_tensor(T.q2[:, :], T.q1[:, 0:64], T.q1[:, 64:128], A.add))
-    w("V", e, e_qm)
-    e = one(V.tensor_tensor(T.qf[:, :], T.q2[:, :], T.qm[:, :], A.add))
-    V.wait_ge(T.sem.x3c, n3c)
-    w("V", e)
-    e_qg = one(V.tensor_tensor(T.qg[:, :], T.qf[:, :], T.rx3[:, 384:448], A.add))
-    V.wait_ge(T.sem.x3b, n3b)
-    e = one(V.tensor_tensor(T.q3[:, :], T.rx3[:, 256:320], T.rx3[:, 320:384], A.add))
-    w("V", e, e_qg)
+    w("P", e_perm, e_vb)
+    for j, (s, slots) in enumerate(((0, (0, 1)), (3, (6,)), (1, (2, 3)), (2, (4, 5)))):
+        P.wait_ge(T.sem["x3" + "abcd"[s]], n3[s])
+        for k in slots:
+            e = mm(T.p2[:, 0:64], T.prm[:, :], T.rx3[:, 64 * k:64 * k + 64], k == 0, k == 5)
+        if j == 2:
+            w("P", e_qm)
+            mm(T.p2[:, 0:64], T.prm[:, :], T.qm[:, :], False, False)
+    e_sum = one(e)
+    w("V", e_sum)
     e_yo = ev()
     for v in range(4):
-        inc(e_yo, V.tensor_tensor(T.yo[:, v:64:4], T.q3[:, 16 * v:16 * v + 16], T.qg[:, 16 * v:16 * v + 16], A.add))
-    e_y = ev()
-    for k in range(8):
-        qn = "YS"[k % 2]
-        n = 65 if k == 7 else 64
-        w(qn, e_yo, e_yc)
-        inc(e_y, names[qn].dma_start(T.y[:, 64 * k:64 * k + n], T.yo[16 * k:16 * k + 16, 0:n]), 16)
+        inc(e_yo, V.tensor_copy(T.yo[:, v:64:4], T.p2[:, 16 * v:16 * v + 16]))
+    w("Y", e_yo, e_y0)
+    e_y = one(Y.dma_start(T.y[:, 0:512], T.yo[:, :]), 16)
     g.wait_ge(T.sem.l0, m0)
     g.wait_ge(T.sem.l1, m1)
     g.wait_ge(T.sem.l2, m2)

@@ -6,36 +6,38 @@ F32, BF, I32, U16 = "float32", "bfloat16", "int32", "uint16"
 WIN = 5120
 ROWS = 16384
 PAD = 96
-NV = 20
-CHUNK = ((640, 640, 640), (1152, 1152, 1152))
+NV = 18
+CHUNK = ((256, 256, 256), (768, 768, 768), (816, 816, 816))
 OWN = ROWS - sum(map(sum, CHUNK))
-EARLY = 1024
+EARLY = 4096
+SERVED = (0, 1, 2, 6, 3, 4, 5)
 LN2 = math.log(2.0)
 SCRATCH = {}
 for _t, _list in (
-        (BF, "f1 128,f2 128,pall 136,onesb 128,negb 128,wp 16,we 16,wm 16,idb 128,tri 128,qs0 8,qs 8,"
-             "bb 256,rb 256,win8 1024,gw 4096,tt 128,sc 128,msk 128,cum 32,vb 512,win 5120,sel 8,pm 128,"
+        (BF, "f1 128,f2 128,pall 272,onesb 128,wp 32,wm 32,onesw 288,tri 128,qs0 8,qs 8,"
+             "bb 256,rb 256,wa 1024,wb 1024,gw 4096,tt 128,sc 128,msk 128,cum 32,vb 512,win 5120,sel 8,pm 128,"
              "lh0 128,lh1 128,hb 256,qt 32"),
-        (I32, "a0 128,im 16,im2 16,iv 16,iv2 16,fks 256,wi 256,u0 128,u1 128,v0 128,v1 128,mn 512,"
-              "ml 32,ml2 32,at2 16480,vr 256,od 1"),
-        (F32, "onesf 128,ivf 16,xj 32,rt 256,e1 32,e2 32,ga 512,rx3 448,qm 64,kf 256,lk0 128,lk1 128,"
-              "mv 512,vbf 512,win2 5120,mwin 5120,b7 240,yo 64,yc 2,prm 128,m16 16,self 8,bz 1"),
+        (I32, "a0 128,im 16,im2 16,iv 32,iv2 32,fks 512,u0 128,u1 128,v0 128,v1 128,"
+              "ml 32,ml2 32,at2 16480,vr 256,od 1,i8 8,j8 8"),
+        ("float16", "wh 256"),
+        (F32, "onesf 128,two 8,k8 8,pw 8,xj 32,rt 256,e1 32,e2 32,ga 512,rx3 448,qm 64,kf 256,lk0 128,lk1 128,"
+              "mv 512,vbf 512,win2 5120,mwin 5120,b7 240,yo 64,yc 2,prm 128,m16 16,self 8,bz 2"),
         (U16, "w16 256,off 32,off2 32,ml16 32,z16 32")):
     for _x in _list.split(","):
         SCRATCH[_x.split()[0]] = ("sbuf", [128, int(_x.split()[1])], _t)
-for _t in range(2):
+for _t in range(len(CHUNK)):
     for _i in range(3):
         SCRATCH["hd%d%d" % (_t, _i)] = ("dram", [128, CHUNK[_t][_i] // 8], I32)
         SCRATCH["raw%d%d" % (_t, _i)] = ("dram", [128, CHUNK[_t][_i] // 8], I32)
-for _t in range(2):
     SCRATCH["hw%d" % _t] = ("sbuf", [128, max(CHUNK[_t])], I32)
+SCRATCH["slf"] = ("sbuf", [128, 18, 16], BF)
 SCRATCH["lm"] = ("sbuf", [1, 2], I32)
 SCRATCH["lf"] = ("sbuf", [1, 2], F32)
 for _k in range(4):
-    SCRATCH["p%d" % _k] = ("psum", [128, 512], F32)
+    SCRATCH["p%d" % _k] = ("psum", [128, 2, 256] if _k % 2 else [128, 512], F32)
     SCRATCH["t%d" % _k] = ("psum", [128, 1024], BF)
-SEMAPHORES = ["x1", "x2a", "x2b", "x2c", "x2d", "x3a", "x3b", "x3c", "x3d", "l0", "l1", "l2", "l3", "hr0", "hr1", "wn", "go"] + [
-    "e%d" % k for k in range(130)]
+SEMAPHORES = ["x10", "x11", "l0", "l1", "l2", "l3", "hr0", "hr1", "hr2", "wn", "go"] + [
+    "x%d%d" % (x, k) for x in (2, 3) for k in range(7)] + ["e%d" % k for k in range(120)]
 
 
 def helpers(core, T, topo):
@@ -62,7 +64,8 @@ def distance_order(core, T, topo):
         return 2 if topo.same_plane(ch, here) else 3
     out = []
     for ch in sorted(chips, key=lambda ch: (-far(ch), (ch - here) % len(chips))):
-        out.append((ch, [r for r in range(len(T.cores)) if topo.chip(T.cores[r]) == ch]))
+        rs = [r for r in range(len(T.cores)) if topo.chip(T.cores[r]) == ch]
+        out.append((ch, sorted(rs, key=lambda r: topo.die(T.cores[r]) != topo.die(core), reverse=far(ch) == 1)))
     return out
 
 
@@ -85,10 +88,13 @@ def plans(core, T, topo):
     far = [r for ch, rs in order[:-1] for r in rs]
     near = [r for r in order[-1][1] if r != me]
     eo, en = engine_sets(core, T, topo)
-    x1 = [[(far, eo), (near, en[:2])]]
-    x2 = [[([far[2 * j + k]], eo[4 * k:4 * k + 4]) for k in range(2)] for j in range(3)]
-    x2[1].append((near, en[:4]))
-    return order, x1, x2, x2
+    x1 = [[(far[4:] + near, eo)], [(far[:4], eo)]]
+    half = len(eo) // 2
+    x2 = [[(far[0:1], eo)], [(far[1:2], eo)], [(far[2:3], eo[:half]), (far[3:4], eo[half:]), (near, en)],
+          [(far[4:5], eo[:half]), (far[5:6], eo[half:])]]
+    x3 = [[([r], eo)] for r in far]
+    x3[2].append((near, en))
+    return order, x1, x2, x3
 
 
 def arriving(core, T, topo, which, slots=range(8)):
@@ -111,14 +117,14 @@ def transfer(dest_cores, eng, rsem, src, dst, topo):
                              dsts=[dst] * len(ids))
 
 
-RAW_CALLS = (((0, 0), (0, 1), (0, 2)), ((1, 0), (1, 1), (1, 2)))
+RAW_CALLS = [[(t, i) for i in range(3)] for t in range(len(CHUNK))]
 
 
-def raw_engines(owner, helper, t, i, topo):
-    eng = topo.engines(owner, helper)
+def raw_engines(owner, helper, t, i, T, topo):
+    eng = topo.engines(owner, helper) if t == 0 else engine_sets(owner, T, topo)[1]
     call = [c for c in RAW_CALLS if (t, i) in c][0]
     n = len(eng) >> (len(call) - 1).bit_length()
-    k = call.index((t, i))
+    k = (call.index((t, i)) + 3 * (t == 2)) % 4
     return eng[n * k:n * k + n]
 
 
@@ -128,20 +134,20 @@ def helper_program(g, core, T, topo):
         return
     owner = owners[0]
     i = helpers(owner, T, topo).index(core)
-    for t in range(2):
+    for t in range(len(CHUNK)):
         n = CHUNK[t][i]
         for q in (g.sync, g.scalar):
-            q.wait_ge(T.sem["hr%d" % t], len(raw_engines(owner, core, t, i, topo)))
+            q.wait_ge(T.sem["hr%d" % t], len(raw_engines(owner, core, t, i, T, topo)))
         for k in range(8):
             q = (g.sync, g.scalar)[k % 2]
             q.dma_start(T["hw%d" % t][16 * k:16 * k + 16, 0:n], T["hd%d%d" % (t, i)][:, :]).then_inc(T.sem["e%d" % t], 16)
     eng = topo.engines(core, owner)
-    for t in range(2):
+    for t in range(len(CHUNK)):
         g.wait_ge(T.sem["e%d" % t], 128)
         c0, n = PAD + chunk_start(t, i), CHUNK[t][i]
         g.remote_dma_fused([transfer([owner], eng, T.sem.wn, T["hw%d" % t][:, 0:n], T.at2[:, c0:c0 + n], topo)],
                            local_sem=T.sem.l0)
-    g.wait_ge(T.sem.l0, 2 * len(eng))
+    g.wait_ge(T.sem.l0, len(CHUNK) * len(eng))
 
 
 def rank_program(g, core, T, topo):
@@ -181,11 +187,12 @@ def rank_program(g, core, T, topo):
         return V.tensor_copy(out, in_) if qn == "V" else S.activation(out, in_, Fn.Copy)
 
     order, x1, x2, x3 = plans(core, T, topo)
-    n1 = arriving(core, T, topo, 1)
-    n2 = [arriving(core, T, topo, 2, range(2 * k, 2 * k + 2)) for k in range(4)]
-    n3 = [arriving(core, T, topo, 3, range(2 * k, 2 * k + 2)) for k in range(4)]
+    n1 = [arriving(core, T, topo, 1, s) for s in (range(4, 8), range(4))]
+    first = [min(r for ch, rs in part for r in rs) for part in (order[2:], order[:2])]
+    n2, n3 = [[arriving(core, T, topo, x, [k]) for k in range(7)] for x in (2, 3)]
+    served = SERVED
     hs = helpers(core, T, topo)
-    nw = sum(2 * len(topo.engines(h, core)) for h in hs)
+    nw = sum(len(CHUNK) * len(topo.engines(h, core)) for h in hs)
     m0 = 0
 
     def send(calls, rsem, lsem, src, dst):
@@ -197,7 +204,7 @@ def rank_program(g, core, T, topo):
         return n
 
     def send_raw(call):
-        engs = [raw_engines(core, hs[i], t, i, topo) for t, i in call]
+        engs = [raw_engines(core, hs[i], t, i, T, topo) for t, i in call]
         g.remote_dma_fused([transfer([hs[i]], eng, T.sem["hr%d" % t], T["raw%d%d" % (t, i)][:, :],
                                      T["hd%d%d" % (t, i)][:, :], topo) for (t, i), eng in zip(call, engs)],
                            local_sem=T.sem.l0)
@@ -216,164 +223,181 @@ def rank_program(g, core, T, topo):
 
     e_lim = one(S.dma_start(T.lm[:, :], T.lim[:, :]), 16)
     e_a0 = one(Y.dma_start(T.a0[:, :], T["at"][0:1, :]), 16)
-    e_raw = [raw_load((S, Y), RAW_CALLS[0])]
-    e_fk = one(Y.dma_start(T.fks[:, :], T.fk[:, :]), 16)
-    e_mn0 = one(V.memset(T.mn[:, :], 0))
-    w("Y", e_mn0)
-    e_mn = one(Y.dma_start(T.mn[0::16, :], T["me"][0:1, :]), 16)
+    e_raw = [raw_load((Y,), RAW_CALLS[0])]
+    e_fk = one(S.dma_start(T.fks[:, 0:256], T.fk[:, :]), 16)
+    e_raw += [raw_load((Y,), call) for call in RAW_CALLS[1:]]
     e_vr = ev()
     for k in range(8):
         inc(e_vr, Y.dma_start(T.vr[16 * k:16 * k + 16, :], T.fk[:, 32 * k:32 * k + 32]), 16)
-    e_raw += [raw_load((Y,), call) for call in RAW_CALLS[1:]]
 
-    e_ivf = one(g.iota(T.ivf[:, :], [[-64, 2], [-1, 8]], 0, 1, allow_small_or_imprecise_dtypes=True))
-    e_iv = one(g.iota(T.iv[:, :], [[-64, 2], [-1, 8]], 0, 1))
+    e_i8 = one(g.iota(T.i8[:, :], [[8, 8]], -56, 1))
+    e_iv = one(g.iota(T.iv[:, :], [[0, 2], [-64, 2], [-1, 8]], 0, 1))
     e_im = one(g.iota(T.im[:, :], [[-1, 16]], 0, 1))
     e_ml = one(g.iota(T.ml[:, :], [[1, 32]], 0, 32))
-    e_onesb = one(V.memset(T.onesb[:, :], 1.0))
     e_onesf = one(V.memset(T.onesf[:, :], 1.0))
-    e_pt = one(V.memset(T.pall[:, 128:136], 0.0))
-    w("S", e_ivf)
-    e_we = one(S.activation(T.we[:, :], T.ivf[:, :], Fn.Exp, scale=LN2 / 8))
+    e_onesw = one(V.memset(T.onesw[:, :], 1.0))
+    e_two = one(V.memset(T.two[:, :], 2.0))
+    e_slot = one(V.memset(T.at2[:, 0:PAD], 0))
+    w("S", e_onesf)
+    e_onesb = one(S.activation(T.onesb[:, :], T.onesf[:, :], Fn.Exp, scale=0.0))
+    w("g", e_onesw)
+    e_slf = one(g.affine_select(T.slf[:, :, :], T.onesw[:, :], [[-16, 9], [1000, 2], [-1, 16]], A.is_equal, 0.0, -1000, 1))
+    ident = T.slf[:, 1:17:2, :]
+    w("V", e_i8)
+    e_j8 = one(V.tensor_scalar(T.j8[:, :], T.i8[:, :], 0x38, None, A.bitwise_and))
     w("V", e_iv)
     e_iv2 = one(V.tensor_scalar(T.iv2[:, :], T.iv[:, :], 0x7FFFFFC7, None, A.bitwise_and))
-    w("V", e_im)
-    e_im2 = one(V.tensor_scalar(T.im2[:, :], T.im[:, :], 15, None, A.bitwise_and))
-    e_slot = one(V.memset(T.at2[:, 0:PAD], 0))
-    e_od = one(V.tensor_scalar(T.od[:, :], T.im[:, 0:1], 1, None, A.bitwise_and))
-    e_qt = one(V.memset(T.qt[:, :], 0.25))
+    w("V", e_j8)
+    e_k8 = one(V.tensor_scalar(T.k8[:, :], T.j8[:, :], 0.0, None, A.is_equal))
     w("V", e_iv2)
     e_wm = one(V.tensor_scalar(T.wm[:, :], T.iv2[:, :], 0.0, None, A.is_equal))
-    w("V", e_ml)
+    w("V", e_k8, e_two)
+    e_pw = one(V.tensor_tensor_scan(T.pw[:, :], T.two[:, :], T.k8[:, :], 0.0, A.mult, A.add))
+    e_pt = ev()
+    for ph in range(2):
+        inc(e_pt, V.memset(T.pall[:, 136 * ph + 128:136 * ph + 136], 0.0))
+    w("V", e_wm, e_pw)
+    e_w = one(V.tensor_scalar(T.wp[:, :], T.wm[:, :], T.pw[:, 7:8], None, A.mult))
+    w("V", e_im, e_ml)
+    e_im2 = one(V.tensor_scalar(T.im2[:, :], T.im[:, :], 15, None, A.bitwise_and))
+    e_od = one(V.tensor_scalar(T.od[:, :], T.im[:, 0:1], 1, None, A.bitwise_and))
     e_ml2 = one(V.tensor_scalar(T.ml2[:, :], T.ml[:, :], 511, None, A.bitwise_and))
-    w("V", e_im2)
-    e_m16 = one(V.tensor_scalar(T.m16[:, :], T.im2[:, :], 0.0, None, A.is_equal))
-    w("V", e_ml2)
-    e_ml16 = one(V.tensor_copy(T.ml16[:, :], T.ml2[:, :]))
-    w("V", e_od, e_m16)
-    e_bz = one(V.tensor_scalar(T.bz[:, :], T.od[:, :], 64.0, None, A.mult))
-    e_sel = ev()
-    for t in (T.sel, T["self"]):
-        inc(e_sel, V.tensor_tensor(t[:, :], T.m16[:, 0::2], T.m16[:, 1::2], A.add))
-    w("V", e_wm, e_we)
-    e_w = one(V.tensor_tensor(T.wp[:, :], T.we[:, :], T.wm[:, :], A.mult))
-    w("g", e_onesb)
-    e_id = one(g.affine_select(T.idb[:, :], T.onesb[:, :], [[-1, 128]], A.is_equal, 0.0, 0, 1))
-    e_pm = one(g.iota(T.pm[:, :], [[0, 64], [-2, 2]], 1, 0, allow_small_or_imprecise_dtypes=True))
-    w("S", e_onesf)
-    e_win0 = ev()
-    for k in range(4):
-        inc(e_win0, S.activation(T.win[:, 128 * k:128 * k + 128], T.onesf[:, :], Fn.Copy, scale=0.0))
-    w("S", e_ml16, e_mn)
-    e_mv = one(S.activation(T.mv[:, :], T.mn[:, :].indirect(T.ml16[:, 0:32]), Fn.Copy))
+    e_qt = one(V.memset(T.qt[:, :], 0.25))
+    e_pm = ev()
+    for k in range(2):
+        inc(e_pm, V.memset(T.pm[:, k::2], 1.0 - 2 * k))
 
-    w("g", e_raw[0])
-    m0 += send_raw(RAW_CALLS[0])
+    for k, call in enumerate(RAW_CALLS):
+        w("g", e_raw[k])
+        m0 += send_raw(call)
 
     w("V", e_lim)
     e_lf = one(V.tensor_copy(T.lf[:, :], T.lm[:, :]))
     w("P", e_lf, e_onesf)
     e_lp = one(mm(T.p0[:, 0:2], T.onesf[0:1, :], T.lf[:, :]))
+    w("V", e_im2, e_ml2, e_od)
+    e_m16 = one(V.tensor_scalar(T.m16[:, :], T.im2[:, :], 0.0, None, A.is_equal))
+    e_ml16 = one(V.tensor_copy(T.ml16[:, :], T.ml2[:, :]))
     w("V", e_lp, e_a0)
     e_f1 = one(V.tensor_scalar(T.f1[:, :], T.a0[:, :], T.p0[:, 0:1], None, A.is_lt))
     e_f2 = one(V.tensor_scalar(T.f2[:, :], T.a0[:, :], T.p0[:, 1:2], None, A.is_gt))
     w("V", e_fk)
-    e_bb = one(V.tensor_scalar(T.bb[:, :], T.fks[:, :], 163840.0 - 511.5, None, A.add))
+    e_wi = one(V.tensor_scalar(T.fks[:, 256:512], T.fks[:, 0:256], 1023, None, A.bitwise_and))
+    w("S", e_fk)
+    e_bb = one(S.activation(T.bb[:, :], T.fks[:, 0:256], Fn.Identity, bias=163840.0 - 511.5))
     w("P", e_w, e_f1)
-    mm(T.p3[:, 0:16], T.f1[:, :], T.wp[:, :], True, False)
+    mm(T.p3[:, 0, 0:32], T.f1[:, :], T.wp[:, :], True, False)
     w("P", e_f2)
-    e_pk = one(mm(T.p3[:, 0:16], T.f2[:, :], T.wp[:, :], False, True))
+    e_pk = one(mm(T.p3[:, 0, 0:32], T.f2[:, :], T.wp[:, :], False, True))
     w("V", e_pk)
-    slot1 = T.pall[:, 16 * me:16 * me + 16]
-    e_pall = one(V.tensor_copy(slot1, T.p3[:, 0:16]))
+    slot1 = [T.pall[:, 136 * ph + 32 * (me - first[0]):136 * ph + 32 * (me - first[0]) + 32] for ph in range(2)]
+    e_pall = one(V.tensor_copy(slot1[0], T.p3[:, 0, 0:32]))
+    w("V", e_wi)
+    e_wh = one(V.tensor_copy(T.wh[:, :], T.fks[:, 256:512]))
 
     w("g", e_pall)
-    m1 = send(x1, lambda r: T.sem.x1, T.sem.l1, lambda r: slot1, lambda r: slot1)
+    m1 = 0
+    for ph in range(2):
+        m1 += send(x1[ph:ph + 1], lambda r: T.sem["x1%d" % ph], T.sem.l1, lambda r: slot1[0], lambda r: slot1[ph])
     g.sem_inc(T.sem.go, 1)
-    for k in range(1, len(RAW_CALLS)):
-        w("g", e_raw[k])
-        m0 += send_raw(RAW_CALLS[k])
 
     w("Y", e_slot)
     e_at = ev()
-    if EARLY:
-        own_load(e_at, 0, EARLY, range(8))
+    own_load(e_at, 0, EARLY, range(1))
     Y.wait_ge(T.sem.go, 1)
-    own_load(e_at, EARLY, OWN, range(8))
+    own_load(e_at, EARLY, OWN, range(1))
+    w("Y", e_wh, e_bb)
+    e_mn = one(Y.dma_start(T.fks[0::16, :], T["me"][0:1, :]), 16)
+    own_load(e_at, 0, OWN, range(1, 8))
 
-    e_lh = ev()
-    w("g", e_pm, e_onesf)
-    for x in range(2):
-        inc(e_lh, g.affine_select(T["lh%d" % x][:, :], T.pm[:, :], [[-2, 64], [0, 2]], A.is_equal, 0.0, -x, 1))
-        inc(e_lh, g.affine_select(T["lk%d" % x][:, :], T.onesf[:, :], [[-2, 64], [1000, 2]], A.is_equal, 0.0,
-                                  -x - 1000, 1))
-    e_qs0 = one(g.affine_select(T.qs0[:, :], T.onesb[:, 0:8], [[-16, 8]], A.is_equal, 0.0, 0, 1))
-    w("g", e_qs0)
-    e_qs = one(g.affine_select(T.qs[:, :], T.qs0[:, :], [[-16, 8]], A.not_equal, 256.0, -8, 1))
-    e_msk = one(g.affine_select(T.msk[:, :], T.onesb[:, :], [[0, 32], [1, 4]], A.not_equal, 0.0, 0, 0))
-    e_tri = one(g.affine_select(T.tri[:, :], T.onesb[:, :], [[1, 128]], A.is_gt, 0.0, 0, -1))
-    e_xj = one(g.iota(T.xj[:, :], [[1, 32]], 513, 32, allow_small_or_imprecise_dtypes=True))
-    e_negb = one(g.iota(T.negb[:, :], [[0, 128]], -1, 0, allow_small_or_imprecise_dtypes=True))
-    e_b70 = one(g.iota(T.b7[:, :], [[0, 240]], 1, 0, allow_small_or_imprecise_dtypes=True))
-    w("g", e_b70)
-    e_b7 = one(g.affine_select(T.b7[:, :], T.b7[:, :], [[1, 15], [0, 16]], A.is_equal, 0.0, -7, 0))
-    e_perm = one(g.affine_select(T.prm[:, :], T.onesf[:, :], [[-1, 16], [-16, 8]], A.is_equal, 0.0, 0, 1))
-
-    e_wi = one(V.tensor_scalar(T.wi[:, :], T.fks[:, :], 1023, None, A.bitwise_and))
-    w("V", e_wi)
-    e_w16 = ev()
-    for h in range(2):
-        inc(e_w16, V.tensor_copy(T.w16[:, 128 * h:128 * h + 128], T.wi[:, h::2]))
-    w("S", e_bb)
-    e_rb = one(S.activation(T.rb[:, :], T.bb[:, :], Fn.Exp, bias=175 * LN2, scale=-LN2 / 1024))
-    e_win20 = ev()
-    for k in range(4):
-        inc(e_win20, S.activation(T.win2[:, 128 * k:128 * k + 128], T.onesf[:, :], Fn.Silu, scale=0.0))
-    w("P", e_rb, e_id)
-    e_rp = ev()
-    for h in range(2):
-        for d in range(8):
-            inc(e_rp, mm(T.p1[:, 128 * h + d:128 * h + 128:8], T.rb[:, h::2], T.idb[:, 16 * d:16 * d + 16]))
-    w("V", e_vr)
+    w("g", e_pm, e_onesf, e_vr)
     e_kf = ev()
     for t in (T.kf, T.hb):
-        inc(e_kf, V.tensor_scalar(t[:, :], T.vr[:, :], 32.0, None, A.add))
-    w("V", e_rp)
-    e_rt = one(V.tensor_copy(T.rt[:, :], T.p1[:, 0:256]))
+        inc(e_kf, g.affine_select(t[:, :], T.vr[:, :], [[0, 256]], A.is_equal, 0.0, 0, 0))
+    e_lh = [ev(), ev()]
+    for x in range(2):
+        inc(e_lh[x], g.affine_select(T["lh%d" % x][:, :], T.pm[:, :], [[-2, 64], [0, 2]], A.is_equal, 0.0, -x, 1))
+        inc(e_lh[x], g.affine_select(T["lk%d" % x][:, :], T.onesf[:, :], [[-2, 64], [1000, 2]], A.is_equal, 0.0,
+                                     -x - 1000, 1))
+    e_msk = one(g.affine_select(T.msk[:, :], T.onesf[:, :], [[0, 32], [1, 4]], A.not_equal, 0.0, 0, 0))
+    e_tri = one(g.affine_select(T.tri[:, :], T.onesf[:, :], [[1, 128]], A.is_gt, 0.0, 0, -1))
+    e_xj = one(g.iota(T.xj[:, :], [[1, 32]], 513, 32, allow_small_or_imprecise_dtypes=True))
+    e_win0 = one(g.iota(T.win[:, 0:512], [[0, 512]], 0, 0, allow_small_or_imprecise_dtypes=True))
+    e_perm = one(g.affine_select(T.prm[:, :], T.onesf[:, :], [[-1, 16], [-16, 8]], A.is_equal, 0.0, 0, 1))
 
-    P.wait_ge(T.sem.x1, n1)
+    w("P", e_wh, e_slf, e_f2)
+    lists = (T.p2[:, 0:128], T.p0[:, 64:192])
+    e_w16 = []
+    for ph in range(2):
+        s = slice(16 * first[ph], 16 * first[ph] + 64)
+        for h in range(2):
+            e = mm(lists[ph], T.slf[s, 2 * first[ph] + 1 - h:2 * first[ph] + 9 - h, :], T.wh[s, h::2], h == 0, h == 1)
+        w("V", one(e))
+        e_w16.append(one(V.tensor_copy(T.w16[:, 128 * ph:128 * ph + 128], lists[ph])))
+    w("S", e_bb)
+    e_rb = one(S.activation(T.rb[:, :], T.bb[:, :], Fn.Exp, bias=175 * LN2, scale=-LN2 / 1024))
+    e_win20 = one(S.activation(T.win2[:, 0:64], T.bb[:, 0:64], Fn.Silu, scale=0.0))
+    w("P", e_rb)
+    e_rp = ev()
+    for ph in range(2):
+        for h in range(2):
+            for i in range(4):
+                d = first[ph] + i
+                inc(e_rp, mm(T.p1[:, ph, 64 * h + i:64 * h + 64:4], T.rb[:, h::2], T.slf[:, 2 * d + 1, :]))
+    w("V", e_slf)
+    e_qs = ev()
+    for h in range(2):
+        inc(e_qs, V.tensor_scalar(T.qs0[:, 4 * h:4 * h + 4], T.slf[:, 2 * h + 1:17:4, 8], 256.0, None, A.mult))
+    w("V", e_m16, e_qs)
+    e_qs = ev()
+    for h in range(2):
+        inc(e_qs, V.tensor_tensor(T.qs[:, 4 * h:4 * h + 4], T.qs0[:, 4 * h:4 * h + 4], T.slf[:, 2 * h + 1:17:4, 0], A.add))
+    e_sel = ev()
+    for t in (T.sel, T["self"]):
+        inc(e_sel, V.tensor_tensor(t[:, :], T.m16[:, 0::2], T.m16[:, 1::2], A.add))
+    e_bz = ev()
+    inc(e_bz, V.tensor_scalar(T.bz[:, 0:1], T.od[:, :], float(PAD), None, A.mult))
+    inc(e_bz, V.tensor_scalar(T.bz[:, 1:2], T.od[:, :], PAD - 64.0, 32.0, A.mult, A.add))
+    w("V", e_rp)
+    e_rt = one(V.tensor_copy(T.rt[:, :], T.p1[:, :, 0:128]))
+
     w("P", e_pall, e_pt)
-    e_w8 = ev()
-    k = 0
-    for j, (qn, n) in enumerate((("S", 2), ("V", 3), ("S", 1), ("V", 2))):
-        bank = T["t%d" % j]
-        e = ev()
-        for m in range(n):
-            inc(e, P.transpose(bank[:, 128 * m:128 * m + 128], T.pall[:, k + m:k + m + 128], T.idb[:, :]))
-        w(qn, e)
-        inc(e_w8, copy(qn, T.win8[:, 128 * k:128 * (k + n)], bank[:, 0:128 * n]))
-        k += n
-    w("V", e_w8, e_w16)
-    w("S", e_w8, e_w16)
     e_g = [ev(), ev()]
-    for h in range(2):
-        for half in range(2):
-            k = 2 * h + half
-            src = T.win8[:, :].indirect(T.w16[:, 64 * k:64 * k + 64])
-            inc(e_g[h], copy("VS"[half], T.gw[:, 1024 * k:1024 * k + 1024], src))
-    w("P", e_kf, e_lh)
+    e_free = {}
+    for ph, pieces in enumerate(((("V", 3, 0), ("V", 3, 1), ("V", 2, 2)), (("V", 5, 3), ("S", 3, 0)))):
+        wph = (T.wa, T.wb)[ph]
+        P.wait_ge(T.sem["x1%d" % ph], n1[ph])
+        e_w8 = []
+        k = 0
+        for qn, n, j in pieces:
+            bank = T["t%d" % j]
+            if j in e_free:
+                w("P", e_free[j])
+            e = ev()
+            for m in range(n):
+                c0 = 136 * ph + k + m
+                inc(e, P.transpose(bank[:, 128 * m:128 * m + 128], T.pall[:, c0:c0 + 128], ident))
+            w(qn, e)
+            e_free[j] = one(copy(qn, wph[:, 128 * k:128 * (k + n)], bank[:, 0:128 * n]))
+            e_w8.append(e_free[j])
+            k += n
+        cut = 128 * ph + 64
+        for qn, c0, c1 in (("V", 128 * ph, cut), ("S", cut, 128 * ph + 128)):
+            w(qn, e_w16[ph], *e_w8)
+            inc(e_g[ph], copy(qn, T.gw[:, 16 * c0:16 * c1], wph[:, :].indirect(T.w16[:, c0:c1])))
+    w("P", e_kf, e_w16[0])
     e_vp = ev()
-    for h in range(2):
-        for x in range(2):
+    for x in range(2):
+        w("P", e_lh[x])
+        for h in range(2):
             out = T.p2[:, 256 * h + 128 * x:256 * h + 128 * x + 128]
             mm(out, T["lh%d" % x][:, :], T.hb[:, h::2], True, False)
             inc(e_vp, mm(out, T["lk%d" % x][:, :], T.kf[:, h::2], False, True))
     w("S", e_vp, e_bz)
     e_vb = one(S.activation(T.vb[:, 0:16 * NV], T.p2[:, 0:16 * NV], Fn.Identity, bias=T.bz[:, 0:1]))
-    e_vbf = one(S.activation(T.vbf[:, 16 * NV:512], T.p2[:, 16 * NV:512], Fn.Identity, bias=T.bz[:, 0:1]))
-    e_mw0 = ev()
-    for k in range(4):
-        inc(e_mw0, S.activation(T.mwin[:, 128 * k:128 * k + 128], T.onesf[:, :], Fn.Copy, scale=0.0))
+    e_vbf = one(S.activation(T.vbf[:, 16 * NV:512], T.p2[:, 16 * NV:512], Fn.Identity, bias=T.bz[:, 1:2]))
+    w("S", e_g[0])
+    inc(e_win20, S.activation(T.win2[:, 64:512], T.gw[:, 0:448], Fn.Silu, scale=0.0))
 
     w("P", e_qs, e_rt, e_pall)
     e_tt = ev()
@@ -382,14 +406,14 @@ def rank_program(g, core, T, topo):
         w("P", e_g[h])
         e = ev()
         for p in range(16):
-            inc(e, mm(bank[:, 8 * p:8 * p + 8], T.gw[:, 2048 * h + p:2048 * h + 2048:16], T.qs[:, :]))
+            inc(e, mm(bank[:, :, 4 * p:4 * p + 4], T.gw[:, 2048 * h + p:2048 * h + 2048:16], T.qs[:, :]))
         w("V", e, e_rt)
         u, v = T["u%d" % h], T["v%d" % h]
-        e = one(V.tensor_tensor(u[:, :], bank[:, 0:128], T.rt[:, 128 * h:128 * h + 128], A.mult))
+        e = one(V.tensor_tensor(u[:, :], bank[:, :, 0:64], T.rt[:, 128 * h:128 * h + 128], A.mult))
         w("V", e)
         e = one(V.tensor_scalar(v[:, :], u[:, :], 15, 1, A.logical_shift_right, A.bitwise_and))
         w("V", e)
-        inc(e_tt, V.tensor_tensor(T.tt[:, 64 * h:64 * h + 64], v[:, 0::2], v[:, 1::2], A.max))
+        inc(e_tt, V.tensor_tensor(T.tt[:, h::2], v[:, 0::2], v[:, 1::2], A.max))
     w("V", e_tt, e_msk)
     e_ns = one(V.tensor_tensor_scan(T.sc[:, :], T.msk[:, :], T.tt[:, :], 0.0, A.mult, A.max))
     ns = T.sc[:, 3:128:4]
@@ -404,21 +428,23 @@ def rank_program(g, core, T, topo):
     e_e2 = one(V.tensor_tensor(T.e2[:, :], T.e1[:, :], T.cum[:, :], A.subtract))
     w("V", e_base, e_e2)
     e_off = one(V.tensor_scalar(T.off[:, :], T.e2[:, :], T.p0[:, 16:17], 1.0, A.subtract, A.subtract))
-    w("P", e_off, e_negb)
-    e_cnt = one(mm(T.p0[:, 32:34], T.negb[:, :], T.cum[:, 30:32]))
+    w("P", e_off, e_onesb)
+    e_cnt = one(mm(T.p0[:, 32:34], T.onesb[:, :], T.cum[:, 30:32]))
     w("V", e_off, e_vb, e_win0)
-    e_sc = one(V.tensor_copy(T.win[:, 0:WIN].indirect(T.off[:, 0:NV]), T.vb[:, 0:16 * NV]))
+    e_sc = one(V.tensor_copy(T.win[:, :].indirect(T.off[:, 0:NV]), T.vb[:, 0:16 * NV]))
     w("S", e_off, e_vbf, e_win20)
-    e_sc2 = one(S.activation(T.win2[:, 0:WIN].indirect(T.off[:, NV:32]), T.vbf[:, 16 * NV:512], Fn.Silu))
-    w("P", e_qt, e_sel)
-    mm(T.p3[:, 128:160], T.onesb[0:1, :], T.qt[0:1, :], True, False)
+    e_sc2 = one(S.activation(T.win2[:, :].indirect(T.off[:, NV:32]), T.vbf[:, 16 * NV:512], Fn.Silu))
+    w("S", e_ml16, e_mn)
+    e_mv = one(S.activation(T.mv[:, :], T.fks[:, :].indirect(T.ml16[:, 0:32]), Fn.Copy))
+    w("P", e_qt, e_sel, e_onesb)
+    mm(T.p3[:, 0, 128:160], T.onesb[0:1, :], T.qt[0:1, :], True, False)
     for e, win, sel in ((e_sc2, T.win2, T["self"]), (e_sc, T.win, T.sel)):
         w("P", e)
         for b in range(4):
-            last = mm(T.p3[:, 128 + b:160:4], win[:, b:512:4], sel[:, :], False, e == e_sc and b == 3)
+            last = mm(T.p3[:, 0, 128 + b:160:4], win[:, b:512:4], sel[:, :], False, e == e_sc and b == 3)
     e_ls = one(last)
     w("V", e_ls)
-    e_z = one(V.tensor_copy(T.z16[:, :], T.p3[:, 128:160]))
+    e_z = one(V.tensor_copy(T.z16[:, :], T.p3[:, 0, 128:160]))
 
     w("g", e_z)
 
@@ -427,64 +453,64 @@ def rank_program(g, core, T, topo):
         return T.off2[:, 4 * k:4 * k + 4]
 
     def sem2(r):
-        return T.sem["x2" + "abcd"[slot_of(r, me, T, topo) // 2]]
+        return T.sem["x2%d" % slot_of(r, me, T, topo)]
     m2 = send(x2, sem2, T.sem.l2, lambda r: T.z16[:, 4 * r:4 * r + 4], land2)
 
     w("V", e_cnt)
-    e_yc = one(V.tensor_copy(T.yc[:, :], T.p0[:, 32:34]))
+    e_yc = one(V.tensor_scalar(T.yc[:, :], T.p0[:, 32:34], -1.0, None, A.mult))
+    e_mw0 = one(V.memset(T.mwin[:, 0:512], 0.0))
+    e_b7 = ev()
+    for c0, c1 in ((0, 112), (128, 240)):
+        inc(e_b7, V.memset(T.b7[:, c0:c1], 0.0))
+    inc(e_b7, V.tensor_scalar(T.b7[:, 112:128], T.onesf[:, 0:16], T.m16[:, 0:1], None, A.mult))
     w("Y", e_yc)
     e_y0 = one(Y.dma_start(T.y[:, 511:513], T.yc[0:16, :]), 16)
     w("V", e_mv, e_mw0)
-    e_ms1 = one(V.tensor_copy(T.mwin[:, 0:WIN].indirect(T.off[:, 0:16]), T.mv[:, 0:256]))
+    e_ms = one(V.tensor_copy(T.mwin[:, 0:WIN].indirect(T.off[:, 0:32]), T.mv[:, :]))
     window = T.at2[:, :]
     w("S", e_z, e_at)
     S.wait_ge(T.sem.wn, nw)
-    e_own3 = one(copy("S", T.ga[:, 448:512], window.indirect(T.z16[:, 4 * me:4 * me + 4])))
 
-    V.wait_ge(T.sem.wn, nw)
-    w("V", e_at)
-    e_ga = [ev() for call in x3]
-    for j, qn, k in ((0, "V", 0), (0, "S", 1), (1, "V", 2), (1, "S", 3), (1, "S", 6), (2, "V", 4), (2, "S", 5)):
-        names[qn].wait_ge(T.sem["x2" + "abcd"[k // 2]], n2[k // 2])
-        inc(e_ga[j], copy(qn, T.ga[:, 64 * k:64 * k + 64], window.indirect(T.off2[:, 4 * k:4 * k + 4])))
+    e_ga = {}
+    for k in served:
+        S.wait_ge(T.sem["x2%d" % k], n2[k])
+        e_ga[k] = one(copy("S", T.ga[:, 64 * k:64 * k + 64], window.indirect(T.off2[:, 4 * k:4 * k + 4])))
+        if k == served[1]:
+            e_own3 = one(copy("S", T.ga[:, 448:512], window.indirect(T.z16[:, 4 * me:4 * me + 4])))
 
     def land3(r):
         k = slot_of(r, me, T, topo)
         return T.rx3[:, 64 * k:64 * k + 64]
 
     def sem3(r):
-        return T.sem["x3" + "abcd"[slot_of(r, me, T, topo) // 2]]
+        return T.sem["x3%d" % slot_of(r, me, T, topo)]
 
     def block(r):
         k = slot_of(me, r, T, topo)
         return T.ga[:, 64 * k:64 * k + 64]
     m3 = 0
-    for k, call in enumerate(x3):
-        w("g", e_ga[k])
+    for call in x3:
+        w("g", *[e_ga[slot_of(me, dests[0], T, topo)] for dests, eng in call])
         m3 += send([call], sem3, T.sem.l3, block, land3)
 
-    w("V", e_ms1)
-    e_ms = one(V.tensor_copy(T.mwin[:, 0:WIN].indirect(T.off[:, 16:32]), T.mv[:, 256:512]))
     w("P", e_ms, e_b7)
     for k in range(8):
-        e = mm(T.p1[:, 0:64], T.b7[:, 112 - 16 * k:240 - 16 * k], T.mwin[:, 64 * k:64 * k + 64], k == 0, k == 7)
+        e = mm(T.p1[:, 0, 0:64], T.b7[:, 112 - 16 * k:240 - 16 * k], T.mwin[:, 64 * k:64 * k + 64], k == 0, k == 7)
     e_mm = one(e)
     w("V", e_mm, e_own3)
     e_qm = ev()
     for v in range(4):
-        inc(e_qm, V.tensor_tensor(T.qm[:, 16 * v:16 * v + 16], T.p1[:, v:64:4],
+        inc(e_qm, V.tensor_tensor(T.qm[:, 16 * v:16 * v + 16], T.p1[:, 0, v:64:4],
                                   T.ga[:, 448 + 16 * v:464 + 16 * v], A.add))
 
-    w("P", e_perm, e_vb)
-    for j, (s, slots) in enumerate(((0, (0, 1)), (3, (6,)), (1, (2, 3)), (2, (4, 5)))):
-        P.wait_ge(T.sem["x3" + "abcd"[s]], n3[s])
-        for k in slots:
-            e = mm(T.p2[:, 0:64], T.prm[:, :], T.rx3[:, 64 * k:64 * k + 64], k == 0, k == 5)
-        if j == 2:
+    w("P", e_perm, e_vb, e_vbf)
+    for k in served:
+        P.wait_ge(T.sem["x3%d" % k], n3[k])
+        e = mm(T.p2[:, 0:64], T.prm[:, :], T.rx3[:, 64 * k:64 * k + 64], k == served[0], k == served[-1])
+        if k == served[-2]:
             w("P", e_qm)
             mm(T.p2[:, 0:64], T.prm[:, :], T.qm[:, :], False, False)
-    e_sum = one(e)
-    w("V", e_sum)
+    w("V", one(e))
     e_yo = ev()
     for v in range(4):
         inc(e_yo, V.tensor_copy(T.yo[:, v:64:4], T.p2[:, 16 * v:16 * v + 16]))

import math
from concourse.bass import DstId, RemoteDMATransfer
from concourse.mybir import AluOpType as A, ActivationFunctionType as Fn

F32, BF, I32, U16 = "float32", "bfloat16", "int32", "uint16"
WIN = 5120
ROWS = 16384
PAD = 96
NV = 18
CHUNK = ((256, 256, 256), (768, 768, 768), (816, 816, 816))
OWN = ROWS - sum(map(sum, CHUNK))
EARLY = 4096
SERVED = (0, 1, 2, 6, 3, 4, 5)
LN2 = math.log(2.0)
SCRATCH = {}
for _t, _list in (
        (BF, "f1 128,f2 128,pall 272,onesb 128,wp 32,wm 32,onesw 288,tri 128,qs0 8,qs 8,"
             "bb 256,rb 256,wa 1024,wb 1024,gw 4096,tt 128,sc 128,msk 128,cum 32,vb 512,win 5120,sel 8,pm 128,"
             "lh0 128,lh1 128,hb 256,qt 32"),
        (I32, "a0 128,im 16,im2 16,iv 32,iv2 32,fks 512,u0 128,u1 128,v0 128,v1 128,"
              "ml 32,ml2 32,at2 16480,vr 256,od 1,i8 8,j8 8"),
        ("float16", "wh 256"),
        (F32, "onesf 128,two 8,k8 8,pw 8,xj 32,rt 256,e1 32,e2 32,ga 512,rx3 448,qm 64,kf 256,lk0 128,lk1 128,"
              "mv 512,vbf 512,win2 5120,mwin 5120,b7 240,yo 64,yc 2,prm 128,m16 16,self 8,bz 2"),
        (U16, "w16 256,off 32,off2 32,ml16 32,z16 32")):
    for _x in _list.split(","):
        SCRATCH[_x.split()[0]] = ("sbuf", [128, int(_x.split()[1])], _t)
for _t in range(len(CHUNK)):
    for _i in range(3):
        SCRATCH["hd%d%d" % (_t, _i)] = ("dram", [128, CHUNK[_t][_i] // 8], I32)
        SCRATCH["raw%d%d" % (_t, _i)] = ("dram", [128, CHUNK[_t][_i] // 8], I32)
    SCRATCH["hw%d" % _t] = ("sbuf", [128, max(CHUNK[_t])], I32)
SCRATCH["slf"] = ("sbuf", [128, 18, 16], BF)
SCRATCH["lm"] = ("sbuf", [1, 2], I32)
SCRATCH["lf"] = ("sbuf", [1, 2], F32)
for _k in range(4):
    SCRATCH["p%d" % _k] = ("psum", [128, 2, 256] if _k % 2 else [128, 512], F32)
    SCRATCH["t%d" % _k] = ("psum", [128, 1024], BF)
SEMAPHORES = ["x10", "x11", "l0", "l1", "l2", "l3", "hr0", "hr1", "hr2", "wn", "go"] + [
    "x%d%d" % (x, k) for x in (2, 3) for k in range(7)] + ["e%d" % k for k in range(120)]


def helpers(core, T, topo):
    hs = [c for c in topo.cores_of(core) if c not in T.cores and topo.die(c) == topo.die(core)]
    return hs[:3]


def chunk_start(t, i):
    return OWN + sum(sum(c) for c in CHUNK[:t]) + sum(CHUNK[t][:i])


def distance_order(core, T, topo):
    here = topo.chip(core)
    chips = []
    for c in T.cores:
        if topo.chip(c) not in chips:
            chips.append(topo.chip(c))

    def far(ch):
        if ch == here:
            return 0
        if topo.mates(ch, here):
            return 1
        return 2 if topo.same_plane(ch, here) else 3
    out = []
    for ch in sorted(chips, key=lambda ch: (-far(ch), (ch - here) % len(chips))):
        rs = [r for r in range(len(T.cores)) if topo.chip(T.cores[r]) == ch]
        out.append((ch, sorted(rs, key=lambda r: topo.die(T.cores[r]) != topo.die(core), reverse=far(ch) == 1)))
    return out


def slot_of(rank, sender, T, topo):
    flat = [r for ch, rs in distance_order(T.cores[rank], T, topo) for r in rs if r != rank] + [rank]
    return flat.index(sender)


def engine_sets(core, T, topo):
    me = T.rank_of(core)
    order = distance_order(core, T, topo)
    near = [r for r in order[-1][1] if r != me]
    eo = topo.engines(core, T.cores[order[0][1][0]])
    return eo, [e for e in topo.engines(core, T.cores[near[0]]) if e not in eo]


def plans(core, T, topo):
    me = T.rank_of(core)
    order = distance_order(core, T, topo)
    far = [r for ch, rs in order[:-1] for r in rs]
    near = [r for r in order[-1][1] if r != me]
    eo, en = engine_sets(core, T, topo)
    x1 = [[(far[4:] + near, eo)], [(far[:4], eo)]]
    half = len(eo) // 2
    x2 = [[(far[0:1], eo)], [(far[1:2], eo)], [(far[2:3], eo[:half]), (far[3:4], eo[half:]), (near, en)],
          [(far[4:5], eo[:half]), (far[5:6], eo[half:])]]
    x3 = [[([r], eo)] for r in far]
    x3[2].append((near, en))
    return order, x1, x2, x3


def arriving(core, T, topo, which, slots=range(8)):
    me, n = T.rank_of(core), 0
    for c in T.cores:
        if c != core and slot_of(me, T.rank_of(c), T, topo) in slots:
            for call in plans(c, T, topo)[which]:
                for dests, eng in call:
                    if me in dests:
                        n += len(eng)
    return n


def transfer(dest_cores, eng, rsem, src, dst, topo):
    ids = []
    for c in dest_cores:
        rid, pid, se = topo.addr(c)
        ids.append(DstId(rid=rid, pnc=pid))
    return RemoteDMATransfer(dst_ids=ids, dma_engine_mask=sum(1 << e for e in eng), remote_sem=rsem, srcs=[src],
                             dsts=[dst] * len(ids))


RAW_CALLS = [[(t, i) for i in range(3)] for t in range(len(CHUNK))]


def raw_engines(owner, helper, t, i, T, topo):
    eng = topo.engines(owner, helper) if t == 0 else engine_sets(owner, T, topo)[1]
    call = [c for c in RAW_CALLS if (t, i) in c][0]
    n = len(eng) >> (len(call) - 1).bit_length()
    k = (call.index((t, i)) + 3 * (t == 2)) % 4
    return eng[n * k:n * k + n]


def helper_program(g, core, T, topo):
    owners = [c for c in T.cores if core in helpers(c, T, topo)]
    if not owners:
        return
    owner = owners[0]
    i = helpers(owner, T, topo).index(core)
    for t in range(len(CHUNK)):
        n = CHUNK[t][i]
        for q in (g.sync, g.scalar):
            q.wait_ge(T.sem["hr%d" % t], len(raw_engines(owner, core, t, i, T, topo)))
        for k in range(8):
            q = (g.sync, g.scalar)[k % 2]
            q.dma_start(T["hw%d" % t][16 * k:16 * k + 16, 0:n], T["hd%d%d" % (t, i)][:, :]).then_inc(T.sem["e%d" % t], 16)
    eng = topo.engines(core, owner)
    for t in range(len(CHUNK)):
        g.wait_ge(T.sem["e%d" % t], 128)
        c0, n = PAD + chunk_start(t, i), CHUNK[t][i]
        g.remote_dma_fused([transfer([owner], eng, T.sem.wn, T["hw%d" % t][:, 0:n], T.at2[:, c0:c0 + n], topo)],
                           local_sem=T.sem.l0)
    g.wait_ge(T.sem.l0, len(CHUNK) * len(eng))


def rank_program(g, core, T, topo):
    me = T.rank_of(core)
    if me is None:
        helper_program(g, core, T, topo)
        return
    V, S, P, Y = g.vector, g.scalar, g.tensor, g.sync
    names = {"g": g, "V": V, "S": S, "P": P, "Y": Y}
    evs = []
    known = {k: [] for k in names}
    waited = []

    def ev():
        evs.append(0)
        return len(evs) - 1

    def inc(e, ins, n=1):
        ins.then_inc(T.sem["e%d" % e], n)
        evs[e] += n
        return e

    def one(ins, n=1):
        return inc(ev(), ins, n)

    def w(qn, *es):
        for e in es:
            if e not in known[qn]:
                names[qn].wait_ge(T.sem["e%d" % e], evs[e])
                known[qn].append(e)
                waited.append(e)

    def mm(out, lhsT, rhs, start=True, stop=True):
        return P.matmul(out, lhsT, rhs, start, stop)

    def copy(qn, out, in_):
        return V.tensor_copy(out, in_) if qn == "V" else S.activation(out, in_, Fn.Copy)

    order, x1, x2, x3 = plans(core, T, topo)
    n1 = [arriving(core, T, topo, 1, s) for s in (range(4, 8), range(4))]
    first = [min(r for ch, rs in part for r in rs) for part in (order[2:], order[:2])]
    n2, n3 = [[arriving(core, T, topo, x, [k]) for k in range(7)] for x in (2, 3)]
    served = SERVED
    hs = helpers(core, T, topo)
    nw = sum(len(CHUNK) * len(topo.engines(h, core)) for h in hs)
    m0 = 0

    def send(calls, rsem, lsem, src, dst):
        n = 0
        for call in calls:
            g.remote_dma_fused([transfer([T.cores[r] for r in dests], eng, rsem(dests[0]), src(dests[0]), dst(dests[0]),
                                         topo) for dests, eng in call], local_sem=lsem)
            n += sum(len(eng) for dests, eng in call)
        return n

    def send_raw(call):
        engs = [raw_engines(core, hs[i], t, i, T, topo) for t, i in call]
        g.remote_dma_fused([transfer([hs[i]], eng, T.sem["hr%d" % t], T["raw%d%d" % (t, i)][:, :],
                                     T["hd%d%d" % (t, i)][:, :], topo) for (t, i), eng in zip(call, engs)],
                           local_sem=T.sem.l0)
        return sum(map(len, engs))

    def raw_load(queues, call):
        e = ev()
        for k, (t, i) in enumerate(call):
            c0 = chunk_start(t, i)
            inc(e, queues[k % len(queues)].dma_start(T["raw%d%d" % (t, i)][:, :], T["at"][:, c0:c0 + CHUNK[t][i]]), 16)
        return e

    def own_load(e, c0, c1, groups):
        for k in groups:
            inc(e, Y.dma_start(T.at2[16 * k:16 * k + 16, PAD + c0:PAD + c1], T["at"][:, c0:c1]), 16)

    e_lim = one(S.dma_start(T.lm[:, :], T.lim[:, :]), 16)
    e_a0 = one(Y.dma_start(T.a0[:, :], T["at"][0:1, :]), 16)
    e_raw = [raw_load((Y,), RAW_CALLS[0])]
    e_fk = one(S.dma_start(T.fks[:, 0:256], T.fk[:, :]), 16)
    e_raw += [raw_load((Y,), call) for call in RAW_CALLS[1:]]
    e_vr = ev()
    for k in range(8):
        inc(e_vr, Y.dma_start(T.vr[16 * k:16 * k + 16, :], T.fk[:, 32 * k:32 * k + 32]), 16)

    e_i8 = one(g.iota(T.i8[:, :], [[8, 8]], -56, 1))
    e_iv = one(g.iota(T.iv[:, :], [[0, 2], [-64, 2], [-1, 8]], 0, 1))
    e_im = one(g.iota(T.im[:, :], [[-1, 16]], 0, 1))
    e_ml = one(g.iota(T.ml[:, :], [[1, 32]], 0, 32))
    e_onesf = one(V.memset(T.onesf[:, :], 1.0))
    e_onesw = one(V.memset(T.onesw[:, :], 1.0))
    e_two = one(V.memset(T.two[:, :], 2.0))
    e_slot = one(V.memset(T.at2[:, 0:PAD], 0))
    w("S", e_onesf)
    e_onesb = one(S.activation(T.onesb[:, :], T.onesf[:, :], Fn.Exp, scale=0.0))
    w("g", e_onesw)
    e_slf = one(g.affine_select(T.slf[:, :, :], T.onesw[:, :], [[-16, 9], [1000, 2], [-1, 16]], A.is_equal, 0.0, -1000, 1))
    ident = T.slf[:, 1:17:2, :]
    w("V", e_i8)
    e_j8 = one(V.tensor_scalar(T.j8[:, :], T.i8[:, :], 0x38, None, A.bitwise_and))
    w("V", e_iv)
    e_iv2 = one(V.tensor_scalar(T.iv2[:, :], T.iv[:, :], 0x7FFFFFC7, None, A.bitwise_and))
    w("V", e_j8)
    e_k8 = one(V.tensor_scalar(T.k8[:, :], T.j8[:, :], 0.0, None, A.is_equal))
    w("V", e_iv2)
    e_wm = one(V.tensor_scalar(T.wm[:, :], T.iv2[:, :], 0.0, None, A.is_equal))
    w("V", e_k8, e_two)
    e_pw = one(V.tensor_tensor_scan(T.pw[:, :], T.two[:, :], T.k8[:, :], 0.0, A.mult, A.add))
    e_pt = ev()
    for ph in range(2):
        inc(e_pt, V.memset(T.pall[:, 136 * ph + 128:136 * ph + 136], 0.0))
    w("V", e_wm, e_pw)
    e_w = one(V.tensor_scalar(T.wp[:, :], T.wm[:, :], T.pw[:, 7:8], None, A.mult))
    w("V", e_im, e_ml)
    e_im2 = one(V.tensor_scalar(T.im2[:, :], T.im[:, :], 15, None, A.bitwise_and))
    e_od = one(V.tensor_scalar(T.od[:, :], T.im[:, 0:1], 1, None, A.bitwise_and))
    e_ml2 = one(V.tensor_scalar(T.ml2[:, :], T.ml[:, :], 511, None, A.bitwise_and))
    e_qt = one(V.memset(T.qt[:, :], 0.25))
    e_pm = ev()
    for k in range(2):
        inc(e_pm, V.memset(T.pm[:, k::2], 1.0 - 2 * k))

    for k, call in enumerate(RAW_CALLS):
        w("g", e_raw[k])
        m0 += send_raw(call)

    w("V", e_lim)
    e_lf = one(V.tensor_copy(T.lf[:, :], T.lm[:, :]))
    w("P", e_lf, e_onesf)
    e_lp = one(mm(T.p0[:, 0:2], T.onesf[0:1, :], T.lf[:, :]))
    w("V", e_im2, e_ml2, e_od)
    e_m16 = one(V.tensor_scalar(T.m16[:, :], T.im2[:, :], 0.0, None, A.is_equal))
    e_ml16 = one(V.tensor_copy(T.ml16[:, :], T.ml2[:, :]))
    w("V", e_lp, e_a0)
    e_f1 = one(V.tensor_scalar(T.f1[:, :], T.a0[:, :], T.p0[:, 0:1], None, A.is_lt))
    e_f2 = one(V.tensor_scalar(T.f2[:, :], T.a0[:, :], T.p0[:, 1:2], None, A.is_gt))
    w("V", e_fk)
    e_wi = one(V.tensor_scalar(T.fks[:, 256:512], T.fks[:, 0:256], 1023, None, A.bitwise_and))
    w("S", e_fk)
    e_bb = one(S.activation(T.bb[:, :], T.fks[:, 0:256], Fn.Identity, bias=163840.0 - 511.5))
    w("P", e_w, e_f1)
    mm(T.p3[:, 0, 0:32], T.f1[:, :], T.wp[:, :], True, False)
    w("P", e_f2)
    e_pk = one(mm(T.p3[:, 0, 0:32], T.f2[:, :], T.wp[:, :], False, True))
    w("V", e_pk)
    slot1 = [T.pall[:, 136 * ph + 32 * (me - first[0]):136 * ph + 32 * (me - first[0]) + 32] for ph in range(2)]
    e_pall = one(V.tensor_copy(slot1[0], T.p3[:, 0, 0:32]))
    w("V", e_wi)
    e_wh = one(V.tensor_copy(T.wh[:, :], T.fks[:, 256:512]))

    w("g", e_pall)
    m1 = 0
    for ph in range(2):
        m1 += send(x1[ph:ph + 1], lambda r: T.sem["x1%d" % ph], T.sem.l1, lambda r: slot1[0], lambda r: slot1[ph])
    g.sem_inc(T.sem.go, 1)

    w("Y", e_slot)
    e_at = ev()
    own_load(e_at, 0, EARLY, range(1))
    Y.wait_ge(T.sem.go, 1)
    own_load(e_at, EARLY, OWN, range(1))
    w("Y", e_wh, e_bb)
    e_mn = one(Y.dma_start(T.fks[0::16, :], T["me"][0:1, :]), 16)
    own_load(e_at, 0, OWN, range(1, 8))

    w("g", e_pm, e_onesf, e_vr)
    e_kf = ev()
    for t in (T.kf, T.hb):
        inc(e_kf, g.affine_select(t[:, :], T.vr[:, :], [[0, 256]], A.is_equal, 0.0, 0, 0))
    e_lh = [ev(), ev()]
    for x in range(2):
        inc(e_lh[x], g.affine_select(T["lh%d" % x][:, :], T.pm[:, :], [[-2, 64], [0, 2]], A.is_equal, 0.0, -x, 1))
        inc(e_lh[x], g.affine_select(T["lk%d" % x][:, :], T.onesf[:, :], [[-2, 64], [1000, 2]], A.is_equal, 0.0,
                                     -x - 1000, 1))
    e_msk = one(g.affine_select(T.msk[:, :], T.onesf[:, :], [[0, 32], [1, 4]], A.not_equal, 0.0, 0, 0))
    e_tri = one(g.affine_select(T.tri[:, :], T.onesf[:, :], [[1, 128]], A.is_gt, 0.0, 0, -1))
    e_xj = one(g.iota(T.xj[:, :], [[1, 32]], 513, 32, allow_small_or_imprecise_dtypes=True))
    e_win0 = one(g.iota(T.win[:, 0:512], [[0, 512]], 0, 0, allow_small_or_imprecise_dtypes=True))
    e_perm = one(g.affine_select(T.prm[:, :], T.onesf[:, :], [[-1, 16], [-16, 8]], A.is_equal, 0.0, 0, 1))

    w("P", e_wh, e_slf, e_f2)
    lists = (T.p2[:, 0:128], T.p0[:, 64:192])
    e_w16 = []
    for ph in range(2):
        s = slice(16 * first[ph], 16 * first[ph] + 64)
        for h in range(2):
            e = mm(lists[ph], T.slf[s, 2 * first[ph] + 1 - h:2 * first[ph] + 9 - h, :], T.wh[s, h::2], h == 0, h == 1)
        w("V", one(e))
        e_w16.append(one(V.tensor_copy(T.w16[:, 128 * ph:128 * ph + 128], lists[ph])))
    w("S", e_bb)
    e_rb = one(S.activation(T.rb[:, :], T.bb[:, :], Fn.Exp, bias=175 * LN2, scale=-LN2 / 1024))
    e_win20 = one(S.activation(T.win2[:, 0:64], T.bb[:, 0:64], Fn.Silu, scale=0.0))
    w("P", e_rb)
    e_rp = ev()
    for ph in range(2):
        for h in range(2):
            for i in range(4):
                d = first[ph] + i
                inc(e_rp, mm(T.p1[:, ph, 64 * h + i:64 * h + 64:4], T.rb[:, h::2], T.slf[:, 2 * d + 1, :]))
    w("V", e_slf)
    e_qs = ev()
    for h in range(2):
        inc(e_qs, V.tensor_scalar(T.qs0[:, 4 * h:4 * h + 4], T.slf[:, 2 * h + 1:17:4, 8], 256.0, None, A.mult))
    w("V", e_m16, e_qs)
    e_qs = ev()
    for h in range(2):
        inc(e_qs, V.tensor_tensor(T.qs[:, 4 * h:4 * h + 4], T.qs0[:, 4 * h:4 * h + 4], T.slf[:, 2 * h + 1:17:4, 0], A.add))
    e_sel = ev()
    for t in (T.sel, T["self"]):
        inc(e_sel, V.tensor_tensor(t[:, :], T.m16[:, 0::2], T.m16[:, 1::2], A.add))
    e_bz = ev()
    inc(e_bz, V.tensor_scalar(T.bz[:, 0:1], T.od[:, :], float(PAD), None, A.mult))
    inc(e_bz, V.tensor_scalar(T.bz[:, 1:2], T.od[:, :], PAD - 64.0, 32.0, A.mult, A.add))
    w("V", e_rp)
    e_rt = one(V.tensor_copy(T.rt[:, :], T.p1[:, :, 0:128]))

    w("P", e_pall, e_pt)
    e_g = [ev(), ev()]
    e_free = {}
    for ph, pieces in enumerate(((("V", 3, 0), ("V", 3, 1), ("V", 2, 2)), (("V", 5, 3), ("S", 3, 0)))):
        wph = (T.wa, T.wb)[ph]
        P.wait_ge(T.sem["x1%d" % ph], n1[ph])
        e_w8 = []
        k = 0
        for qn, n, j in pieces:
            bank = T["t%d" % j]
            if j in e_free:
                w("P", e_free[j])
            e = ev()
            for m in range(n):
                c0 = 136 * ph + k + m
                inc(e, P.transpose(bank[:, 128 * m:128 * m + 128], T.pall[:, c0:c0 + 128], ident))
            w(qn, e)
            e_free[j] = one(copy(qn, wph[:, 128 * k:128 * (k + n)], bank[:, 0:128 * n]))
            e_w8.append(e_free[j])
            k += n
        cut = 128 * ph + 64
        for qn, c0, c1 in (("V", 128 * ph, cut), ("S", cut, 128 * ph + 128)):
            w(qn, e_w16[ph], *e_w8)
            inc(e_g[ph], copy(qn, T.gw[:, 16 * c0:16 * c1], wph[:, :].indirect(T.w16[:, c0:c1])))
    w("P", e_kf, e_w16[0])
    e_vp = ev()
    for x in range(2):
        w("P", e_lh[x])
        for h in range(2):
            out = T.p2[:, 256 * h + 128 * x:256 * h + 128 * x + 128]
            mm(out, T["lh%d" % x][:, :], T.hb[:, h::2], True, False)
            inc(e_vp, mm(out, T["lk%d" % x][:, :], T.kf[:, h::2], False, True))
    w("S", e_vp, e_bz)
    e_vb = one(S.activation(T.vb[:, 0:16 * NV], T.p2[:, 0:16 * NV], Fn.Identity, bias=T.bz[:, 0:1]))
    e_vbf = one(S.activation(T.vbf[:, 16 * NV:512], T.p2[:, 16 * NV:512], Fn.Identity, bias=T.bz[:, 1:2]))
    w("S", e_g[0])
    inc(e_win20, S.activation(T.win2[:, 64:512], T.gw[:, 0:448], Fn.Silu, scale=0.0))

    w("P", e_qs, e_rt, e_pall)
    e_tt = ev()
    for h in range(2):
        bank = (T.p1, T.p3)[h]
        w("P", e_g[h])
        e = ev()
        for p in range(16):
            inc(e, mm(bank[:, :, 4 * p:4 * p + 4], T.gw[:, 2048 * h + p:2048 * h + 2048:16], T.qs[:, :]))
        w("V", e, e_rt)
        u, v = T["u%d" % h], T["v%d" % h]
        e = one(V.tensor_tensor(u[:, :], bank[:, :, 0:64], T.rt[:, 128 * h:128 * h + 128], A.mult))
        w("V", e)
        e = one(V.tensor_scalar(v[:, :], u[:, :], 15, 1, A.logical_shift_right, A.bitwise_and))
        w("V", e)
        inc(e_tt, V.tensor_tensor(T.tt[:, h::2], v[:, 0::2], v[:, 1::2], A.max))
    w("V", e_tt, e_msk)
    e_ns = one(V.tensor_tensor_scan(T.sc[:, :], T.msk[:, :], T.tt[:, :], 0.0, A.mult, A.max))
    ns = T.sc[:, 3:128:4]

    w("V", e_ns, e_onesb)
    e_cum = one(V.tensor_tensor_scan(T.cum[:, :], ns, T.onesb[:, 0:32], 0.0, A.add, A.subtract))
    w("P", e_cum, e_tri)
    e_base = one(mm(T.p0[:, 16:17], T.tri[:, :], T.cum[:, 31:32]))
    w("V", e_xj)
    e_e1 = one(V.tensor_tensor(T.e1[:, :], ns, T.xj[:, :], A.mult))
    w("V", e_cum, e_e1)
    e_e2 = one(V.tensor_tensor(T.e2[:, :], T.e1[:, :], T.cum[:, :], A.subtract))
    w("V", e_base, e_e2)
    e_off = one(V.tensor_scalar(T.off[:, :], T.e2[:, :], T.p0[:, 16:17], 1.0, A.subtract, A.subtract))
    w("P", e_off, e_onesb)
    e_cnt = one(mm(T.p0[:, 32:34], T.onesb[:, :], T.cum[:, 30:32]))
    w("V", e_off, e_vb, e_win0)
    e_sc = one(V.tensor_copy(T.win[:, :].indirect(T.off[:, 0:NV]), T.vb[:, 0:16 * NV]))
    w("S", e_off, e_vbf, e_win20)
    e_sc2 = one(S.activation(T.win2[:, :].indirect(T.off[:, NV:32]), T.vbf[:, 16 * NV:512], Fn.Silu))
    w("S", e_ml16, e_mn)
    e_mv = one(S.activation(T.mv[:, :], T.fks[:, :].indirect(T.ml16[:, 0:32]), Fn.Copy))
    w("P", e_qt, e_sel, e_onesb)
    mm(T.p3[:, 0, 128:160], T.onesb[0:1, :], T.qt[0:1, :], True, False)
    for e, win, sel in ((e_sc2, T.win2, T["self"]), (e_sc, T.win, T.sel)):
        w("P", e)
        for b in range(4):
            last = mm(T.p3[:, 0, 128 + b:160:4], win[:, b:512:4], sel[:, :], False, e == e_sc and b == 3)
    e_ls = one(last)
    w("V", e_ls)
    e_z = one(V.tensor_copy(T.z16[:, :], T.p3[:, 0, 128:160]))

    w("g", e_z)

    def land2(r):
        k = slot_of(r, me, T, topo)
        return T.off2[:, 4 * k:4 * k + 4]

    def sem2(r):
        return T.sem["x2%d" % slot_of(r, me, T, topo)]
    m2 = send(x2, sem2, T.sem.l2, lambda r: T.z16[:, 4 * r:4 * r + 4], land2)

    w("V", e_cnt)
    e_yc = one(V.tensor_scalar(T.yc[:, :], T.p0[:, 32:34], -1.0, None, A.mult))
    e_mw0 = one(V.memset(T.mwin[:, 0:512], 0.0))
    e_b7 = ev()
    for c0, c1 in ((0, 112), (128, 240)):
        inc(e_b7, V.memset(T.b7[:, c0:c1], 0.0))
    inc(e_b7, V.tensor_scalar(T.b7[:, 112:128], T.onesf[:, 0:16], T.m16[:, 0:1], None, A.mult))
    w("Y", e_yc)
    e_y0 = one(Y.dma_start(T.y[:, 511:513], T.yc[0:16, :]), 16)
    w("V", e_mv, e_mw0)
    e_ms = one(V.tensor_copy(T.mwin[:, 0:WIN].indirect(T.off[:, 0:32]), T.mv[:, :]))
    window = T.at2[:, :]
    w("S", e_z, e_at)
    S.wait_ge(T.sem.wn, nw)

    e_ga = {}
    for k in served:
        S.wait_ge(T.sem["x2%d" % k], n2[k])
        e_ga[k] = one(copy("S", T.ga[:, 64 * k:64 * k + 64], window.indirect(T.off2[:, 4 * k:4 * k + 4])))
        if k == served[1]:
            e_own3 = one(copy("S", T.ga[:, 448:512], window.indirect(T.z16[:, 4 * me:4 * me + 4])))

    def land3(r):
        k = slot_of(r, me, T, topo)
        return T.rx3[:, 64 * k:64 * k + 64]

    def sem3(r):
        return T.sem["x3%d" % slot_of(r, me, T, topo)]

    def block(r):
        k = slot_of(me, r, T, topo)
        return T.ga[:, 64 * k:64 * k + 64]
    m3 = 0
    for call in x3:
        w("g", *[e_ga[slot_of(me, dests[0], T, topo)] for dests, eng in call])
        m3 += send([call], sem3, T.sem.l3, block, land3)

    w("P", e_ms, e_b7)
    for k in range(8):
        e = mm(T.p1[:, 0, 0:64], T.b7[:, 112 - 16 * k:240 - 16 * k], T.mwin[:, 64 * k:64 * k + 64], k == 0, k == 7)
    e_mm = one(e)
    w("V", e_mm, e_own3)
    e_qm = ev()
    for v in range(4):
        inc(e_qm, V.tensor_tensor(T.qm[:, 16 * v:16 * v + 16], T.p1[:, 0, v:64:4],
                                  T.ga[:, 448 + 16 * v:464 + 16 * v], A.add))

    w("P", e_perm, e_vb, e_vbf)
    for k in served:
        P.wait_ge(T.sem["x3%d" % k], n3[k])
        e = mm(T.p2[:, 0:64], T.prm[:, :], T.rx3[:, 64 * k:64 * k + 64], k == served[0], k == served[-1])
        if k == served[-2]:
            w("P", e_qm)
            mm(T.p2[:, 0:64], T.prm[:, :], T.qm[:, :], False, False)
    w("V", one(e))
    e_yo = ev()
    for v in range(4):
        inc(e_yo, V.tensor_copy(T.yo[:, v:64:4], T.p2[:, 16 * v:16 * v + 16]))
    w("Y", e_yo, e_y0)
    e_y = one(Y.dma_start(T.y[:, 0:512], T.yo[:, :]), 16)
    g.wait_ge(T.sem.l0, m0)
    g.wait_ge(T.sem.l1, m1)
    g.wait_ge(T.sem.l2, m2)
    g.wait_ge(T.sem.l3, m3)
    w("g", e_y)
    for e in range(len(evs)):
        if e not in waited:
            w("g", e)
